import numpy as np
import ml_dtypes


def mxq(x, axis, fmt="e4m3"):
    dtype, down = {"e4m3": (ml_dtypes.float8_e4m3fn, 7), "e5m2": (ml_dtypes.float8_e5m2, 14)}[fmt]
    v = np.moveaxis(np.asarray(x, np.float32).astype(ml_dtypes.bfloat16).astype(np.float64), axis, -1)
    blocks = v.reshape(v.shape[:-1] + (-1, 32))
    amax = np.abs(blocks).max(-1, keepdims=True)
    byte = np.maximum(np.where(amax > 0, np.frexp(amax)[1] - 1 + 127, 0) - down, 1)
    scale = np.exp2(byte - 127.0)
    codes = (blocks / scale).astype(np.float32).astype(dtype).astype(np.float64)
    return np.moveaxis((codes * scale).reshape(v.shape), -1, axis)


WIDE = False


def mx_kscale(k):
    if not WIDE:
        return np.ones(k)
    levels = np.array([18, -18])
    if k % 512:
        return np.exp2(np.random.permutation(np.resize(levels, k // 32))).repeat(32)
    a = np.empty((k // 512, 16))
    for p in range(k // 512):
        a[p, :8] = np.random.permutation(np.resize(levels, 8))
        for g in range(8):
            far = levels[np.abs(levels - a[p, g]) >= 10]
            a[p, g + 8] = far[np.random.randint(len(far))]
    return np.exp2(a.ravel()).repeat(32)


def f64(x):
    return np.asarray(x).astype(np.float64)


def striped(idx):
    return np.tile(np.asarray(idx).reshape(-1, 16).T, (8, 1)).astype(np.uint16)


def unstriped(offs):
    return offs[:16].T.reshape(-1).astype(np.int64)

def planes(y):
    n, m = y.shape
    v = y.astype(np.float32).astype(ml_dtypes.bfloat16).astype(np.float64).reshape(n // 32, 32, m)
    top = np.abs(v).max(1)
    byte = np.clip(np.where(top > 0, np.frexp(top)[1] - 1 + 127 - 7, 1), 1, 254)
    codes = (v * np.exp2(127.0 - byte)[:, None, :]).reshape(n, m).astype(np.float32).astype(ml_dtypes.float8_e4m3fn).view(np.uint8)
    words = codes.reshape(n // 512, 128, 4, m).transpose(0, 1, 3, 2)
    return np.ascontiguousarray(words), np.ascontiguousarray(byte.astype(np.uint8).reshape(n // 512, 16, m))


N, T, D, V = 512, 2048, 512, 512


def setup_inputs():
    n = np.random.standard_normal
    idx = np.random.permutation(T)[:N]
    s = mx_kscale(D)[:, None]
    z = mx_kscale(V)[:, None]
    w = n((D, V)) / np.sqrt(D)
    return {
        "xT": (n((D, T)) / s).astype(np.float32),
        "wd": (w * s).astype(np.float32),
        "wv": (w.T / z).astype(np.float32),
        "y": n((V, N)).astype(np.float32),
        "cw": (np.random.uniform(0.5, 1.5, (V, 1)) / np.sqrt(V) * z).astype(np.float32),
        "rw": np.tile(np.random.uniform(0.5, 1.5, N), (128, 1)).astype(np.float32),
        "offs": striped(idx),
    }


def reference(xT, wd, wv, y, cw, rw, offs):
    idx = unstriped(offs)
    a = mxq(f64(wd), 0, "e4m3").T @ mxq(f64(xT)[:, idx], 0, "e4m3")
    q = a - f64(y)
    g = f64(cw) * f64(rw)[:1] * q / (1.0 + q * q)
    dx = mxq(f64(wv), 0, "e4m3").T @ mxq(g, 0, "e5m2")
    gx = np.zeros((D, T))
    gx[:, idx] = dx
    out_0 = gx
    return (out_0,) + planes(out_0)

@@ -1,0 +1,214 @@
+from contextlib import ExitStack
+
+import concourse.mybir as mybir
+from concourse.masks import make_identity
+
+N, T, D, V = 512, 2048, 512, 512
+FLOPS = 2 * 2 * N * D * V
+
+F32 = mybir.dt.float32
+BF16 = mybir.dt.bfloat16
+I32 = mybir.dt.int32
+U32 = mybir.dt.uint32
+U16 = mybir.dt.uint16
+U8 = mybir.dt.uint8
+E4M3 = mybir.dt.float8_e4m3fn_x4
+E5M2 = mybir.dt.float8_e5m2_x4
+ACT = mybir.ActivationFunctionType
+ALU = mybir.AluOpType
+
+P = 128
+LANES = 4
+CHUNK = 128
+WD_VECTOR = 40
+PIECES = (256, 256, 512, 512, 256, 256)
+SCALAR_WEAVES = (4,)
+
+
+def tile_attend_gml_pl_cau_kernel(tc, xT, wd, wv, y, cw, rw, offs, out_0, out_1, out_2):
+    nc = tc.nc
+    with ExitStack() as ctx:
+        keep = ctx.enter_context(tc.tile_pool(name="keep", bufs=1))
+        psum = ctx.enter_context(tc.psum_pool(name="psum", bufs=1))
+
+        def sb(name, shape, dtype, tag=""):
+            return keep.tile(shape, dtype, name=name, tag=tag or name, align_bytes=64)
+
+        offsets = keep.tile([P, N // 16], U16, name="offsets")
+        nc.sync.dma_start(offsets[:], offs)
+
+        cw_sb = sb("cw_sb", [P, LANES], F32)
+        nc.scalar.dma_start(out=cw_sb[:], in_=cw.rearrange("(p t) o -> p (t o)", t=LANES))
+        rw_cols = sb("rw_cols", [P, LANES], F32)
+        nc.scalar.dma_start(out=rw_cols[:], in_=rw[0:1, :].rearrange("o (p j) -> p (o j)", j=LANES))
+        x_rows = xT.rearrange("(p j) t -> p j t", j=LANES)
+        x_plane = [sb("x_plane%d" % j, [P, T], F32) for j in range(LANES)]
+        for j in range(LANES):
+            nc.sync.dma_start(out=x_plane[j][:], in_=x_rows[:, j, :])
+        wd_rows = wd.rearrange("(p j) v -> p j v", j=LANES)
+        wd_half = [sb("wd_half%d" % h, [P, LANES, V // 2], F32) for h in range(2)]
+        for h in range(2):
+            nc.sync.dma_start(out=wd_half[h][:], in_=wd_rows[:, :, h * (V // 2) : (h + 1) * (V // 2)])
+        y_rows = y.rearrange("(p t) i -> p t i", t=LANES)
+        y_half = [sb("y_half%d" % h, [P, LANES, N // 2], F32) for h in range(2)]
+        for h in range(2):
+            nc.sync.dma_start(out=y_half[h][:], in_=y_rows[:, :, h * (N // 2) : (h + 1) * (N // 2)])
+        wv_raw = sb("wv_raw", [P, LANES, D], F32)
+        nc.sync.dma_start(out=wv_raw[:], in_=wv.rearrange("(p t) d -> p t d", t=LANES))
+
+        warm_in = sb("warm_in", [P, 1], F32)
+        warm_out = sb("warm_out", [P, 1], F32)
+        nc.vector.memset(warm_in[:], 1.0)
+        nc.scalar.activation(out=warm_out[:], in_=warm_in[:], func=ACT.Abs_reciprocal_sqrt)
+
+        window = [sb("window%d" % j, [P, T], F32) for j in range(LANES)]
+        for j in range(LANES):
+            nc.vector.memset(window[j][:], 0.0)
+
+        ident = sb("ident", [P, P], F32)
+        make_identity(nc, ident[:])
+        rw_spread = psum.tile([P, LANES, P], F32, name="rw_spread", tag="grad3")
+        for j in range(LANES):
+            nc.tensor.transpose(rw_spread[:, j, :], rw_cols[:, j : j + 1].to_broadcast([P, P]), ident[:])
+        weight_rows = sb("weight_rows", [P, LANES, N], F32)
+        for t in range(LANES):
+            nc.scalar.activation(
+                out=weight_rows[:, t, :].rearrange("p (n j) -> p n j", j=LANES),
+                in_=rw_spread[:].rearrange("p j n -> p n j"),
+                func=ACT.Copy,
+                scale=cw_sb[:, t : t + 1],
+            )
+
+        weight = sb("weight", [P, N, LANES], F32)
+        nc.scalar.copy(out=weight[:], in_=weight_rows[:].rearrange("p t i -> p i t"))
+
+        x_bf = sb("x_bf", [P, N, LANES], BF16)
+        for j in range(LANES):
+            nc.vector.tensor_copy(out=x_bf[:, :, j], in_=x_plane[j][:].indirect(offsets[:]))
+        x_codes = sb("x_codes", [P, N], U32)
+        x_scales = sb("x_scales", [P, N], U8)
+        nc.vector.quantize_mx(out=x_codes[:].bitcast(E4M3), scales=x_scales[:], in_=x_bf[:].rearrange("p i j -> p (i j)"))
+        chunks = [slice(c * CHUNK, (c + 1) * CHUNK) for c in range(N // CHUNK)]
+
+        wd_bf = sb("wd_bf", [P, LANES, P, LANES], BF16)
+        wd_dealt = wd_bf[:].rearrange("p t m j -> p m j t")
+        half_m = P // 2
+        for copy, h, first, last in (
+            (nc.scalar.copy, 0, 0, half_m),
+            (nc.vector.tensor_copy, 1, 0, WD_VECTOR),
+            (nc.scalar.copy, 1, WD_VECTOR, half_m),
+        ):
+            copy(
+                out=wd_dealt[:, h * half_m + first : h * half_m + last, :, :],
+                in_=wd_half[h][:].rearrange("p j (m t) -> p m j t", t=LANES)[:, first:last, :, :],
+            )
+        wd_codes = sb("wd_codes", [P, V], U32)
+        wd_scales = sb("wd_scales", [P, V], U8)
+        for t in range(LANES):
+            head = slice(t * P, (t + 1) * P)
+            nc.vector.quantize_mx(
+                out=wd_codes[:, head].bitcast(E4M3), scales=wd_scales[:, head], in_=wd_bf[:, t, :, :].rearrange("p m j -> p (m j)")
+            )
+
+        g_codes = sb("g_codes", [P, N], U32)
+        g_scales = sb("g_scales", [P, N], U8)
+        resid, damp = [], []
+        for c, cols in enumerate(chunks):
+            scores = psum.tile([P, LANES, CHUNK], F32, name="scores%d" % c)
+            for t in range(LANES):
+                head = slice(t * P, (t + 1) * P)
+                nc.tensor.matmul_mx(
+                    out=scores[:, t, :],
+                    lhsT=wd_codes[:, head].bitcast(E4M3),
+                    lhsT_scale=wd_scales[:, head],
+                    rhs=x_codes[:, cols].bitcast(E4M3),
+                    rhs_scale=x_scales[:, cols],
+                    start=True,
+                    stop=True,
+                )
+            q = sb("q%d" % c, [P, CHUNK, LANES], F32)
+            within = slice((c % 2) * CHUNK, (c % 2 + 1) * CHUNK)
+            nc.vector.tensor_tensor(
+                out=q[:],
+                in0=scores[:].rearrange("p t i -> p i t"),
+                in1=y_half[c // 2][:, :, within].rearrange("p t i -> p i t"),
+                op=ALU.subtract,
+            )
+            q_sq = sb("q_sq%d" % c, [P, CHUNK, LANES], F32)
+            root = sb("root%d" % c, [P, CHUNK, LANES], F32)
+            inv = sb("inv%d" % c, [P, CHUNK, LANES], F32)
+            nc.scalar.activation(out=q_sq[:], in_=q[:], func=ACT.Square)
+            nc.scalar.activation(out=root[:], in_=q_sq[:], func=ACT.Abs_reciprocal_sqrt, bias=1.0)
+            nc.scalar.activation(out=inv[:], in_=root[:], func=ACT.Square)
+            resid.append(q)
+            damp.append(inv)
+        weighted = []
+        for c, cols in enumerate(chunks):
+            h = sb("h%d" % c, [P, CHUNK, LANES], F32)
+            nc.vector.tensor_tensor(out=h[:], in0=resid[c][:], in1=weight[:, cols, :], op=ALU.mult)
+            weighted.append(h)
+        for c, cols in enumerate(chunks):
+            g_bf = sb("g_bf%d" % c, [P, CHUNK, LANES], BF16)
+            nc.vector.tensor_tensor(out=g_bf[:], in0=weighted[c][:], in1=damp[c][:], op=ALU.mult)
+            nc.vector.quantize_mx(out=g_codes[:, cols].bitcast(E5M2), scales=g_scales[:, cols], in_=g_bf[:].rearrange("p i t -> p (i t)"))
+
+        wv_dealt = wv_raw[:].rearrange("p t (m j) -> p m t j", j=LANES)
+        wv_bf = []
+        for h, tag in enumerate(("root3", "inv3")):
+            half = sb("wv_bf%d" % h, [P, 2, P, LANES], BF16, tag=tag)
+            nc.scalar.copy(out=half[:].rearrange("p j m t -> p m t j"), in_=wv_dealt[:, :, :, 2 * h : 2 * h + 2])
+            wv_bf.append(half)
+
+        starts = [sum(PIECES[:k]) for k in range(len(PIECES))]
+        pairs = sb("pairs", [P, 2 * T * 2], BF16)
+        out_rows = out_0.rearrange("(p j) t -> p j t", j=LANES)
+        for j in range(LANES):
+            wv_codes = sb("wv_codes%d" % j, [P, P], U32)
+            wv_scales = sb("wv_scales%d" % j, [P, P], U8)
+            nc.vector.quantize_mx(
+                out=wv_codes[:].bitcast(E4M3), scales=wv_scales[:], in_=wv_bf[j // 2][:, j % 2, :, :].rearrange("p m t -> p (m t)")
+            )
+            grad = psum.tile([P, N], F32, name="grad%d" % j, tag="grad%d" % j)
+            nc.tensor.matmul_mx(
+                out=grad[:],
+                lhsT=wv_codes[:].bitcast(E4M3),
+                lhsT_scale=wv_scales[:],
+                rhs=g_codes[:].bitcast(E5M2),
+                rhs_scale=g_scales[:],
+                start=True,
+                stop=True,
+            )
+            dx = sb("dx%d" % j, [P, N], F32)
+            if j == 0:
+                nc.vector.tensor_copy(out=dx[:], in_=grad[:])
+            else:
+                nc.scalar.copy(out=dx[:], in_=grad[:])
+            nc.vector.tensor_copy(out=window[j][:].indirect(offsets[:]), in_=dx[:])
+            nc.sync.dma_start(out=out_rows[:, j, :], in_=window[j][:])
+
+        out_words = out_1[0].rearrange("p t l -> p (t l)").bitcast(I32)
+        o_scales = sb("o_scales", [P, T], U8)
+        for j in range(LANES):
+            spans = [(0, T)] if j < LANES - 1 else list(zip(starts, PIECES))
+            for first, w in spans:
+                base = (j // 2) * 2 * T + 2 * first + j % 2
+                nc.scalar.copy(out=pairs[:, base : base + 2 * w - 1 : 2], in_=window[j][:, first : first + w])
+        for k, w in enumerate(PIECES):
+            cols = slice(starts[k], starts[k] + w)
+            o_bf = sb("o_bf%d" % k, [P, w * LANES], BF16)
+            word = U32 if k in SCALAR_WEAVES else I32
+            dst = o_bf[:].bitcast(word).rearrange("p (c u) -> p c u", u=2)
+            src = pairs[:].bitcast(word).rearrange("p (u c) -> p u c", u=2)[:, :, cols].rearrange("p u c -> p c u")
+            if k in SCALAR_WEAVES:
+                nc.scalar.copy(out=dst, in_=src)
+            else:
+                nc.vector.tensor_copy(out=dst, in_=src)
+            o_codes = sb("o_codes%d" % k, [P, w], U32)
+            nc.vector.quantize_mx(out=o_codes[:].bitcast(E4M3), scales=o_scales[:, cols], in_=o_bf[:])
+            nc.sync.dma_start(out=out_words[:, cols], in_=o_codes[:].bitcast(I32))
+        for quad in range(4):
+            queue = nc.sync if quad % 2 == 0 else nc.scalar
+            queue.dma_start(
+                out=out_2[0, 4 * quad : 4 * quad + 4, :].bitcast(I32),
+                in_=o_scales[32 * quad : 32 * quad + 4, :].bitcast(I32),
+            )

@@ -20,7 +20,6 @@ ALU = mybir.AluOpType
 P = 128
 LANES = 4
 CHUNK = 128
-WD_VECTOR = 40
 PIECES = (256, 256, 512, 512, 256, 256)
 SCALAR_WEAVES = (4,)
 
@@ -41,18 +40,14 @@ def tile_attend_gml_pl_cau_kernel(tc, xT, wd, wv, y, cw, rw, offs, out_0, out_1,
         nc.scalar.dma_start(out=cw_sb[:], in_=cw.rearrange("(p t) o -> p (t o)", t=LANES))
         rw_cols = sb("rw_cols", [P, LANES], F32)
         nc.scalar.dma_start(out=rw_cols[:], in_=rw[0:1, :].rearrange("o (p j) -> p (o j)", j=LANES))
+        wd_raw = sb("wd_raw", [P, LANES, V], F32)
+        nc.sync.dma_start(out=wd_raw[:], in_=wd.rearrange("(p j) v -> p j v", j=LANES))
         x_rows = xT.rearrange("(p j) t -> p j t", j=LANES)
         x_plane = [sb("x_plane%d" % j, [P, T], F32) for j in range(LANES)]
         for j in range(LANES):
             nc.sync.dma_start(out=x_plane[j][:], in_=x_rows[:, j, :])
-        wd_rows = wd.rearrange("(p j) v -> p j v", j=LANES)
-        wd_half = [sb("wd_half%d" % h, [P, LANES, V // 2], F32) for h in range(2)]
-        for h in range(2):
-            nc.sync.dma_start(out=wd_half[h][:], in_=wd_rows[:, :, h * (V // 2) : (h + 1) * (V // 2)])
-        y_rows = y.rearrange("(p t) i -> p t i", t=LANES)
-        y_half = [sb("y_half%d" % h, [P, LANES, N // 2], F32) for h in range(2)]
-        for h in range(2):
-            nc.sync.dma_start(out=y_half[h][:], in_=y_rows[:, :, h * (N // 2) : (h + 1) * (N // 2)])
+        y_sb = sb("y_sb", [P, LANES, N], F32)
+        nc.sync.dma_start(out=y_sb[:], in_=y.rearrange("(p t) i -> p t i", t=LANES))
         wv_raw = sb("wv_raw", [P, LANES, D], F32)
         nc.sync.dma_start(out=wv_raw[:], in_=wv.rearrange("(p t) d -> p t d", t=LANES))
 
@@ -62,52 +57,41 @@ def tile_attend_gml_pl_cau_kernel(tc, xT, wd, wv, y, cw, rw, offs, out_0, out_1,
         nc.scalar.activation(out=warm_out[:], in_=warm_in[:], func=ACT.Abs_reciprocal_sqrt)
 
         window = [sb("window%d" % j, [P, T], F32) for j in range(LANES)]
-        for j in range(LANES):
-            nc.vector.memset(window[j][:], 0.0)
-
         ident = sb("ident", [P, P], F32)
         make_identity(nc, ident[:])
+        for j in range(LANES):
+            engine = nc.vector if j < LANES // 2 else nc.gpsimd
+            engine.memset(window[j][:], 0.0)
         rw_spread = psum.tile([P, LANES, P], F32, name="rw_spread", tag="grad3")
         for j in range(LANES):
             nc.tensor.transpose(rw_spread[:, j, :], rw_cols[:, j : j + 1].to_broadcast([P, P]), ident[:])
-        weight_rows = sb("weight_rows", [P, LANES, N], F32)
+        weight = sb("weight", [P, LANES, N], F32)
         for t in range(LANES):
             nc.scalar.activation(
-                out=weight_rows[:, t, :].rearrange("p (n j) -> p n j", j=LANES),
+                out=weight[:, t, :].rearrange("p (n j) -> p n j", j=LANES),
                 in_=rw_spread[:].rearrange("p j n -> p n j"),
                 func=ACT.Copy,
                 scale=cw_sb[:, t : t + 1],
             )
 
-        weight = sb("weight", [P, N, LANES], F32)
-        nc.scalar.copy(out=weight[:], in_=weight_rows[:].rearrange("p t i -> p i t"))
+        wd_bf = sb("wd_bf", [P, V, LANES], BF16)
+        nc.scalar.copy(
+            out=wd_bf[:].rearrange("p (t m) j -> p m j t", t=LANES),
+            in_=wd_raw[:].rearrange("p j (m t) -> p m j t", t=LANES),
+        )
+        wd_codes = sb("wd_codes", [P, V], U32)
+        wd_scales = sb("wd_scales", [P, V], U8)
+        nc.vector.quantize_mx(out=wd_codes[:].bitcast(E4M3), scales=wd_scales[:], in_=wd_bf[:].rearrange("p v j -> p (v j)"))
 
         x_bf = sb("x_bf", [P, N, LANES], BF16)
         for j in range(LANES):
             nc.vector.tensor_copy(out=x_bf[:, :, j], in_=x_plane[j][:].indirect(offsets[:]))
         x_codes = sb("x_codes", [P, N], U32)
         x_scales = sb("x_scales", [P, N], U8)
-        nc.vector.quantize_mx(out=x_codes[:].bitcast(E4M3), scales=x_scales[:], in_=x_bf[:].rearrange("p i j -> p (i j)"))
         chunks = [slice(c * CHUNK, (c + 1) * CHUNK) for c in range(N // CHUNK)]
-
-        wd_bf = sb("wd_bf", [P, LANES, P, LANES], BF16)
-        wd_dealt = wd_bf[:].rearrange("p t m j -> p m j t")
-        half_m = P // 2
-        for copy, h, first, last in (
-            (nc.scalar.copy, 0, 0, half_m),
-            (nc.vector.tensor_copy, 1, 0, WD_VECTOR),
-            (nc.scalar.copy, 1, WD_VECTOR, half_m),
-        ):
-            copy(
-                out=wd_dealt[:, h * half_m + first : h * half_m + last, :, :],
-                in_=wd_half[h][:].rearrange("p j (m t) -> p m j t", t=LANES)[:, first:last, :, :],
-            )
-        wd_codes = sb("wd_codes", [P, V], U32)
-        wd_scales = sb("wd_scales", [P, V], U8)
-        for t in range(LANES):
-            head = slice(t * P, (t + 1) * P)
+        for cols in chunks:
             nc.vector.quantize_mx(
-                out=wd_codes[:, head].bitcast(E4M3), scales=wd_scales[:, head], in_=wd_bf[:, t, :, :].rearrange("p m j -> p (m j)")
+                out=x_codes[:, cols].bitcast(E4M3), scales=x_scales[:, cols], in_=x_bf[:, cols, :].rearrange("p i j -> p (i j)")
             )
 
         g_codes = sb("g_codes", [P, N], U32)
@@ -126,17 +110,11 @@ def tile_attend_gml_pl_cau_kernel(tc, xT, wd, wv, y, cw, rw, offs, out_0, out_1,
                     start=True,
                     stop=True,
                 )
-            q = sb("q%d" % c, [P, CHUNK, LANES], F32)
-            within = slice((c % 2) * CHUNK, (c % 2 + 1) * CHUNK)
-            nc.vector.tensor_tensor(
-                out=q[:],
-                in0=scores[:].rearrange("p t i -> p i t"),
-                in1=y_half[c // 2][:, :, within].rearrange("p t i -> p i t"),
-                op=ALU.subtract,
-            )
-            q_sq = sb("q_sq%d" % c, [P, CHUNK, LANES], F32)
-            root = sb("root%d" % c, [P, CHUNK, LANES], F32)
-            inv = sb("inv%d" % c, [P, CHUNK, LANES], F32)
+            q = sb("q%d" % c, [P, LANES, CHUNK], F32)
+            nc.vector.tensor_tensor(out=q[:], in0=scores[:], in1=y_sb[:, :, cols], op=ALU.subtract)
+            q_sq = sb("q_sq%d" % c, [P, LANES, CHUNK], F32)
+            root = sb("root%d" % c, [P, LANES, CHUNK], F32)
+            inv = sb("inv%d" % c, [P, LANES, CHUNK], F32)
             nc.scalar.activation(out=q_sq[:], in_=q[:], func=ACT.Square)
             nc.scalar.activation(out=root[:], in_=q_sq[:], func=ACT.Abs_reciprocal_sqrt, bias=1.0)
             nc.scalar.activation(out=inv[:], in_=root[:], func=ACT.Square)
@@ -144,12 +122,17 @@ def tile_attend_gml_pl_cau_kernel(tc, xT, wd, wv, y, cw, rw, offs, out_0, out_1,
             damp.append(inv)
         weighted = []
         for c, cols in enumerate(chunks):
-            h = sb("h%d" % c, [P, CHUNK, LANES], F32)
-            nc.vector.tensor_tensor(out=h[:], in0=resid[c][:], in1=weight[:, cols, :], op=ALU.mult)
+            h = sb("h%d" % c, [P, LANES, CHUNK], F32)
+            nc.vector.tensor_tensor(out=h[:], in0=resid[c][:], in1=weight[:, :, cols], op=ALU.mult)
             weighted.append(h)
         for c, cols in enumerate(chunks):
             g_bf = sb("g_bf%d" % c, [P, CHUNK, LANES], BF16)
-            nc.vector.tensor_tensor(out=g_bf[:], in0=weighted[c][:], in1=damp[c][:], op=ALU.mult)
+            nc.vector.tensor_tensor(
+                out=g_bf[:].rearrange("p (c i) t -> p c t i", i=4),
+                in0=weighted[c][:].rearrange("p t (c i) -> p c t i", i=4),
+                in1=damp[c][:].rearrange("p t (c i) -> p c t i", i=4),
+                op=ALU.mult,
+            )
             nc.vector.quantize_mx(out=g_codes[:, cols].bitcast(E5M2), scales=g_scales[:, cols], in_=g_bf[:].rearrange("p i t -> p (i t)"))
 
         wv_dealt = wv_raw[:].rearrange("p t (m j) -> p m t j", j=LANES)

@@ -20,8 +20,9 @@ ALU = mybir.AluOpType
 P = 128
 LANES = 4
 CHUNK = 128
-PIECES = (256, 256, 512, 512, 256, 256)
-SCALAR_WEAVES = (4,)
+PIECES = (128, 128, 256, 512, 512, 256, 256)
+SCALAR_WEAVES = (6,)
+STORE_ENDS = (512, 1024, 1536, 1792, 2048)
 
 
 def tile_attend_gml_pl_cau_kernel(tc, xT, wd, wv, y, cw, rw, offs, out_0, out_1, out_2):
@@ -115,7 +116,10 @@ def tile_attend_gml_pl_cau_kernel(tc, xT, wd, wv, y, cw, rw, offs, out_0, out_1,
             q_sq = sb("q_sq%d" % c, [P, LANES, CHUNK], F32)
             root = sb("root%d" % c, [P, LANES, CHUNK], F32)
             inv = sb("inv%d" % c, [P, LANES, CHUNK], F32)
-            nc.scalar.activation(out=q_sq[:], in_=q[:], func=ACT.Square)
+            if c == len(chunks) - 1:
+                nc.vector.tensor_tensor(out=q_sq[:], in0=q[:], in1=q[:], op=ALU.mult)
+            else:
+                nc.scalar.activation(out=q_sq[:], in_=q[:], func=ACT.Square)
             nc.scalar.activation(out=root[:], in_=q_sq[:], func=ACT.Abs_reciprocal_sqrt, bias=1.0)
             nc.scalar.activation(out=inv[:], in_=root[:], func=ACT.Square)
             resid.append(q)
@@ -163,14 +167,19 @@ def tile_attend_gml_pl_cau_kernel(tc, xT, wd, wv, y, cw, rw, offs, out_0, out_1,
             )
             dx = sb("dx%d" % j, [P, N], F32)
             if j == 0:
-                nc.vector.tensor_copy(out=dx[:], in_=grad[:])
+                halves = [slice(h * (N // 2), (h + 1) * (N // 2)) for h in range(2)]
+                for part in halves:
+                    nc.vector.tensor_copy(out=dx[:, part], in_=grad[:, part])
+                for part in halves:
+                    nc.vector.tensor_copy(out=window[j][:].indirect(offsets[:, part.start // 16 : part.stop // 16]), in_=dx[:, part])
             else:
                 nc.scalar.copy(out=dx[:], in_=grad[:])
-            nc.vector.tensor_copy(out=window[j][:].indirect(offsets[:]), in_=dx[:])
+                nc.vector.tensor_copy(out=window[j][:].indirect(offsets[:]), in_=dx[:])
             nc.sync.dma_start(out=out_rows[:, j, :], in_=window[j][:])
 
         out_words = out_1[0].rearrange("p t l -> p (t l)").bitcast(I32)
         o_scales = sb("o_scales", [P, T], U8)
+        o_codes = sb("o_codes", [P, T], U32)
         for j in range(LANES):
             spans = [(0, T)] if j < LANES - 1 else list(zip(starts, PIECES))
             for first, w in spans:
@@ -186,12 +195,10 @@ def tile_attend_gml_pl_cau_kernel(tc, xT, wd, wv, y, cw, rw, offs, out_0, out_1,
                 nc.scalar.copy(out=dst, in_=src)
             else:
                 nc.vector.tensor_copy(out=dst, in_=src)
-            o_codes = sb("o_codes%d" % k, [P, w], U32)
-            nc.vector.quantize_mx(out=o_codes[:].bitcast(E4M3), scales=o_scales[:, cols], in_=o_bf[:])
-            nc.sync.dma_start(out=out_words[:, cols], in_=o_codes[:].bitcast(I32))
-        for quad in range(4):
-            queue = nc.sync if quad % 2 == 0 else nc.scalar
-            queue.dma_start(
-                out=out_2[0, 4 * quad : 4 * quad + 4, :].bitcast(I32),
-                in_=o_scales[32 * quad : 32 * quad + 4, :].bitcast(I32),
-            )
+            nc.vector.quantize_mx(out=o_codes[:, cols].bitcast(E4M3), scales=o_scales[:, cols], in_=o_bf[:])
+            if cols.stop in STORE_ENDS:
+                run = slice(max([0] + [e for e in STORE_ENDS if e < cols.stop]), cols.stop)
+                nc.sync.dma_start(out=out_words[:, run], in_=o_codes[:, run].bitcast(I32))
+        for r in range(4):
+            queue = nc.sync if r % 2 else nc.scalar
+            queue.dma_start(out=out_2[0, r:16:4, :].bitcast(I32), in_=o_scales[r:P:32, :].bitcast(I32))

@@ -41,14 +41,16 @@ def tile_attend_gml_pl_cau_kernel(tc, xT, wd, wv, y, cw, rw, offs, out_0, out_1,
         nc.scalar.dma_start(out=cw_sb[:], in_=cw.rearrange("(p t) o -> p (t o)", t=LANES))
         rw_cols = sb("rw_cols", [P, LANES], F32)
         nc.scalar.dma_start(out=rw_cols[:], in_=rw[0:1, :].rearrange("o (p j) -> p (o j)", j=LANES))
-        wd_raw = sb("wd_raw", [P, LANES, V], F32)
-        nc.sync.dma_start(out=wd_raw[:], in_=wd.rearrange("(p j) v -> p j v", j=LANES))
         x_rows = xT.rearrange("(p j) t -> p j t", j=LANES)
         x_plane = [sb("x_plane%d" % j, [P, T], F32) for j in range(LANES)]
         for j in range(LANES):
             nc.sync.dma_start(out=x_plane[j][:], in_=x_rows[:, j, :])
-        y_sb = sb("y_sb", [P, LANES, N], F32)
-        nc.sync.dma_start(out=y_sb[:], in_=y.rearrange("(p t) i -> p t i", t=LANES))
+        wd_raw = sb("wd_raw", [P, LANES, V], F32)
+        nc.sync.dma_start(out=wd_raw[:], in_=wd.rearrange("(p j) v -> p j v", j=LANES))
+        y_rows = y.rearrange("(p t) i -> p t i", t=LANES)
+        y_half = [sb("y_half%d" % h, [P, LANES, N // 2], F32) for h in range(2)]
+        for h in range(2):
+            nc.sync.dma_start(out=y_half[h][:], in_=y_rows[:, :, h * (N // 2) : (h + 1) * (N // 2)])
         wv_raw = sb("wv_raw", [P, LANES, D], F32)
         nc.sync.dma_start(out=wv_raw[:], in_=wv.rearrange("(p t) d -> p t d", t=LANES))
 
@@ -75,106 +77,140 @@ def tile_attend_gml_pl_cau_kernel(tc, xT, wd, wv, y, cw, rw, offs, out_0, out_1,
                 scale=cw_sb[:, t : t + 1],
             )
 
-        wd_bf = sb("wd_bf", [P, V, LANES], BF16)
-        nc.scalar.copy(
-            out=wd_bf[:].rearrange("p (t m) j -> p m j t", t=LANES),
-            in_=wd_raw[:].rearrange("p j (m t) -> p m j t", t=LANES),
-        )
-        wd_codes = sb("wd_codes", [P, V], U32)
-        wd_scales = sb("wd_scales", [P, V], U8)
-        nc.vector.quantize_mx(out=wd_codes[:].bitcast(E4M3), scales=wd_scales[:], in_=wd_bf[:].rearrange("p v j -> p (v j)"))
-
         x_bf = sb("x_bf", [P, N, LANES], BF16)
         for j in range(LANES):
             nc.vector.tensor_copy(out=x_bf[:, :, j], in_=x_plane[j][:].indirect(offsets[:]))
         x_codes = sb("x_codes", [P, N], U32)
         x_scales = sb("x_scales", [P, N], U8)
-        chunks = [slice(c * CHUNK, (c + 1) * CHUNK) for c in range(N // CHUNK)]
-        for cols in chunks:
-            nc.vector.quantize_mx(
-                out=x_codes[:, cols].bitcast(E4M3), scales=x_scales[:, cols], in_=x_bf[:, cols, :].rearrange("p i j -> p (i j)")
-            )
+        nc.vector.quantize_mx(out=x_codes[:].bitcast(E4M3), scales=x_scales[:], in_=x_bf[:].rearrange("p i j -> p (i j)"))
 
+        wd_dealt = wd_raw[:].rearrange("p j (m t) -> p m j t", t=LANES)
+        wd_codes, wd_scales = [], []
+        for h in range(2):
+            half = sb("wd_bf%d" % h, [P, 2, P, LANES], BF16)
+            if h == 0:
+                nc.vector.tensor_copy(out=half[:].rearrange("p t m j -> p m j t"), in_=wd_dealt[:, :, :, 0:2])
+            else:
+                nc.scalar.copy(out=half[:].rearrange("p t m j -> p m j t"), in_=wd_dealt[:, :, :, 2:4])
+            codes = sb("wd_codes%d" % h, [P, 2 * P], U32)
+            scales = sb("wd_scales%d" % h, [P, 2 * P], U8)
+            nc.vector.quantize_mx(out=codes[:].bitcast(E4M3), scales=scales[:], in_=half[:].rearrange("p t m j -> p (t m j)"))
+            wd_codes.append(codes)
+            wd_scales.append(scales)
+
+        HALF = N // 2
         g_codes = sb("g_codes", [P, N], U32)
         g_scales = sb("g_scales", [P, N], U8)
-        resid, damp = [], []
-        for c, cols in enumerate(chunks):
-            scores = psum.tile([P, LANES, CHUNK], F32, name="scores%d" % c)
-            for t in range(LANES):
-                head = slice(t * P, (t + 1) * P)
-                nc.tensor.matmul_mx(
-                    out=scores[:, t, :],
-                    lhsT=wd_codes[:, head].bitcast(E4M3),
-                    lhsT_scale=wd_scales[:, head],
-                    rhs=x_codes[:, cols].bitcast(E4M3),
-                    rhs_scale=x_scales[:, cols],
-                    start=True,
-                    stop=True,
-                )
-            q = sb("q%d" % c, [P, LANES, CHUNK], F32)
-            nc.vector.tensor_tensor(out=q[:], in0=scores[:], in1=y_sb[:, :, cols], op=ALU.subtract)
-            q_sq = sb("q_sq%d" % c, [P, LANES, CHUNK], F32)
-            root = sb("root%d" % c, [P, LANES, CHUNK], F32)
-            inv = sb("inv%d" % c, [P, LANES, CHUNK], F32)
-            if c == len(chunks) - 1:
-                nc.vector.tensor_tensor(out=q_sq[:], in0=q[:], in1=q[:], op=ALU.mult)
-            else:
-                nc.scalar.activation(out=q_sq[:], in_=q[:], func=ACT.Square)
-            nc.scalar.activation(out=root[:], in_=q_sq[:], func=ACT.Abs_reciprocal_sqrt, bias=1.0)
-            nc.scalar.activation(out=inv[:], in_=root[:], func=ACT.Square)
-            resid.append(q)
-            damp.append(inv)
+        nc.gpsimd.memset(g_codes[:, HALF:], 0)
+        nc.gpsimd.memset(g_scales[:, HALF:], 0)
+        resid = [sb("q%d" % h, [P, LANES, HALF], F32) for h in range(2)]
+        for h in range(2):
+            cols = slice(h * HALF, (h + 1) * HALF)
+            for u in range(2):
+                scores = psum.tile([P, 2, HALF], F32, name="scores%d" % (2 * h + u))
+                for k in range(2):
+                    head = slice(k * P, (k + 1) * P)
+                    nc.tensor.matmul_mx(
+                        out=scores[:, k, :],
+                        lhsT=wd_codes[u][:, head].bitcast(E4M3),
+                        lhsT_scale=wd_scales[u][:, head],
+                        rhs=x_codes[:, cols].bitcast(E4M3),
+                        rhs_scale=x_scales[:, cols],
+                        start=True,
+                        stop=True,
+                    )
+                tiles = slice(2 * u, 2 * u + 2)
+                nc.vector.tensor_tensor(out=resid[h][:, tiles, :], in0=scores[:], in1=y_half[h][:, tiles, :], op=ALU.subtract)
+        damp = []
+        for h in range(2):
+            q_sq = sb("q_sq%d" % h, [P, LANES, HALF], F32)
+            root = sb("root%d" % h, [P, LANES, HALF], F32)
+            for u in range(2):
+                tiles = slice(2 * u, 2 * u + 2)
+                nc.scalar.activation(out=q_sq[:, tiles, :], in_=resid[h][:, tiles, :], func=ACT.Square)
+            for u in range(2):
+                tiles = slice(2 * u, 2 * u + 2)
+                nc.scalar.activation(out=root[:, tiles, :], in_=q_sq[:, tiles, :], func=ACT.Abs_reciprocal_sqrt, bias=1.0)
+            for k in range(2):
+                inv = sb("inv%d" % (2 * h + k), [P, LANES, CHUNK], F32)
+                nc.scalar.activation(out=inv[:], in_=root[:, :, k * CHUNK : (k + 1) * CHUNK], func=ACT.Square)
+                damp.append(inv)
         weighted = []
-        for c, cols in enumerate(chunks):
-            h = sb("h%d" % c, [P, LANES, CHUNK], F32)
-            nc.vector.tensor_tensor(out=h[:], in0=resid[c][:], in1=weight[:, :, cols], op=ALU.mult)
-            weighted.append(h)
-        for c, cols in enumerate(chunks):
-            g_bf = sb("g_bf%d" % c, [P, CHUNK, LANES], BF16)
-            nc.vector.tensor_tensor(
-                out=g_bf[:].rearrange("p (c i) t -> p c t i", i=4),
-                in0=weighted[c][:].rearrange("p t (c i) -> p c t i", i=4),
-                in1=damp[c][:].rearrange("p t (c i) -> p c t i", i=4),
-                op=ALU.mult,
-            )
-            nc.vector.quantize_mx(out=g_codes[:, cols].bitcast(E5M2), scales=g_scales[:, cols], in_=g_bf[:].rearrange("p i t -> p (i t)"))
+        for h in range(2):
+            prod = sb("h%d" % h, [P, LANES, HALF], F32)
+            nc.vector.tensor_tensor(out=prod[:], in0=resid[h][:], in1=weight[:, :, h * HALF : (h + 1) * HALF], op=ALU.mult)
+            weighted.append(prod)
 
         wv_dealt = wv_raw[:].rearrange("p t (m j) -> p m t j", j=LANES)
         wv_bf = []
-        for h, tag in enumerate(("root3", "inv3")):
-            half = sb("wv_bf%d" % h, [P, 2, P, LANES], BF16, tag=tag)
-            nc.scalar.copy(out=half[:].rearrange("p j m t -> p m t j"), in_=wv_dealt[:, :, :, 2 * h : 2 * h + 2])
-            wv_bf.append(half)
+        wv_codes = [sb("wv_codes%d" % j, [P, P], U32) for j in range(LANES)]
+        wv_scales = [sb("wv_scales%d" % j, [P, P], U8) for j in range(LANES)]
+        g_bf = [sb("g_bf%d" % c, [P, CHUNK, LANES], BF16) for c in range(N // CHUNK)]
 
-        starts = [sum(PIECES[:k]) for k in range(len(PIECES))]
-        pairs = sb("pairs", [P, 2 * T * 2], BF16)
-        out_rows = out_0.rearrange("(p j) t -> p j t", j=LANES)
-        for j in range(LANES):
-            wv_codes = sb("wv_codes%d" % j, [P, P], U32)
-            wv_scales = sb("wv_scales%d" % j, [P, P], U8)
-            nc.vector.quantize_mx(
-                out=wv_codes[:].bitcast(E4M3), scales=wv_scales[:], in_=wv_bf[j // 2][:, j % 2, :, :].rearrange("p m t -> p (m t)")
+        def form_g(c):
+            inner = slice((c % 2) * CHUNK, (c % 2 + 1) * CHUNK)
+            nc.vector.tensor_tensor(
+                out=g_bf[c][:].rearrange("p (c i) t -> p c t i", i=4),
+                in0=weighted[c // 2][:, :, inner].rearrange("p t (c i) -> p c t i", i=4),
+                in1=damp[c][:].rearrange("p t (c i) -> p c t i", i=4),
+                op=ALU.mult,
             )
-            grad = psum.tile([P, N], F32, name="grad%d" % j, tag="grad%d" % j)
+
+        def quantise_g(c):
+            cols = slice(c * CHUNK, (c + 1) * CHUNK)
+            nc.vector.quantize_mx(out=g_codes[:, cols].bitcast(E5M2), scales=g_scales[:, cols], in_=g_bf[c][:].rearrange("p i t -> p (i t)"))
+
+        def quantise_wv(j):
+            nc.vector.quantize_mx(
+                out=wv_codes[j][:].bitcast(E4M3), scales=wv_scales[j][:], in_=wv_bf[j // 2][:, j % 2, :, :].rearrange("p m t -> p (m t)")
+            )
+
+        form_g(0)
+        form_g(1)
+        half = sb("wv_bf0", [P, 2, P, LANES], BF16)
+        nc.vector.tensor_copy(out=half[:].rearrange("p j m t -> p m t j"), in_=wv_dealt[:, :, :, 0:2])
+        wv_bf.append(half)
+        quantise_g(0)
+        quantise_g(1)
+        quantise_wv(0)
+
+        def gradient(j, bank):
+            grad = psum.tile([P, N], F32, name="grad_" + bank, tag=bank)
             nc.tensor.matmul_mx(
                 out=grad[:],
-                lhsT=wv_codes[:].bitcast(E4M3),
-                lhsT_scale=wv_scales[:],
+                lhsT=wv_codes[j][:].bitcast(E4M3),
+                lhsT_scale=wv_scales[j][:],
                 rhs=g_codes[:].bitcast(E5M2),
                 rhs_scale=g_scales[:],
                 start=True,
                 stop=True,
             )
-            dx = sb("dx%d" % j, [P, N], F32)
-            if j == 0:
-                halves = [slice(h * (N // 2), (h + 1) * (N // 2)) for h in range(2)]
-                for part in halves:
-                    nc.vector.tensor_copy(out=dx[:, part], in_=grad[:, part])
-                for part in halves:
-                    nc.vector.tensor_copy(out=window[j][:].indirect(offsets[:, part.start // 16 : part.stop // 16]), in_=dx[:, part])
-            else:
-                nc.scalar.copy(out=dx[:], in_=grad[:])
-                nc.vector.tensor_copy(out=window[j][:].indirect(offsets[:]), in_=dx[:])
+            return grad
+
+        early = gradient(0, "scores0")
+        form_g(2)
+        form_g(3)
+        quantise_g(2)
+        quantise_g(3)
+        dx_early = sb("dx_early", [P, HALF], F32, tag="inv2")
+        nc.scalar.copy(out=dx_early[:], in_=early[:, :HALF])
+        half = sb("wv_bf1", [P, 2, P, LANES], BF16, tag="root1")
+        nc.scalar.copy(out=half[:].rearrange("p j m t -> p m t j"), in_=wv_dealt[:, :, :, 2:4])
+        wv_bf.append(half)
+        quantise_wv(1)
+        nc.vector.tensor_copy(out=window[0][:].indirect(offsets[:, : HALF // 16]), in_=dx_early[:])
+        for j in range(2, LANES):
+            quantise_wv(j)
+
+        starts = [sum(PIECES[:k]) for k in range(len(PIECES))]
+        pairs = sb("pairs", [P, 2 * T * 2], BF16)
+        out_rows = out_0.rearrange("(p j) t -> p j t", j=LANES)
+        for j in range(LANES):
+            grad = gradient(j, "grad%d" % j)
+            first = HALF if j == 0 else 0
+            dx = sb("dx%d" % j, [P, N - first], F32)
+            nc.scalar.copy(out=dx[:], in_=grad[:, first:])
+            nc.vector.tensor_copy(out=window[j][:].indirect(offsets[:, first // 16 :]), in_=dx[:])
             nc.sync.dma_start(out=out_rows[:, j, :], in_=window[j][:])
 
         out_words = out_1[0].rearrange("p t l -> p (t l)").bitcast(I32)

@@ -20,8 +20,8 @@ ALU = mybir.AluOpType
 P = 128
 LANES = 4
 CHUNK = 128
-PIECES = (128, 128, 256, 512, 512, 256, 256)
-SCALAR_WEAVES = (6,)
+PIECES = (128, 128, 256, 256, 256, 256, 256, 256, 256)
+SCALAR_WEAVES = (7, 8)
 STORE_ENDS = (512, 1024, 1536, 1792, 2048)
 
 
@@ -63,8 +63,7 @@ def tile_attend_gml_pl_cau_kernel(tc, xT, wd, wv, y, cw, rw, offs, out_0, out_1,
         ident = sb("ident", [P, P], F32)
         make_identity(nc, ident[:])
         for j in range(LANES):
-            engine = nc.vector if j < LANES // 2 else nc.gpsimd
-            engine.memset(window[j][:], 0.0)
+            nc.vector.memset(window[j][:], 0.0)
         rw_spread = psum.tile([P, LANES, P], F32, name="rw_spread", tag="grad3")
         for j in range(LANES):
             nc.tensor.transpose(rw_spread[:, j, :], rw_cols[:, j : j + 1].to_broadcast([P, P]), ident[:])
@@ -101,8 +100,8 @@ def tile_attend_gml_pl_cau_kernel(tc, xT, wd, wv, y, cw, rw, offs, out_0, out_1,
         HALF = N // 2
         g_codes = sb("g_codes", [P, N], U32)
         g_scales = sb("g_scales", [P, N], U8)
-        nc.gpsimd.memset(g_codes[:, HALF:], 0)
-        nc.gpsimd.memset(g_scales[:, HALF:], 0)
+        nc.vector.memset(g_codes[:, HALF:], 0)
+        nc.vector.memset(g_scales[:, HALF:], 0)
         resid = [sb("q%d" % h, [P, LANES, HALF], F32) for h in range(2)]
         for h in range(2):
             cols = slice(h * HALF, (h + 1) * HALF)
@@ -221,17 +220,24 @@ def tile_attend_gml_pl_cau_kernel(tc, xT, wd, wv, y, cw, rw, offs, out_0, out_1,
             for first, w in spans:
                 base = (j // 2) * 2 * T + 2 * first + j % 2
                 nc.scalar.copy(out=pairs[:, base : base + 2 * w - 1 : 2], in_=window[j][:, first : first + w])
-        for k, w in enumerate(PIECES):
-            cols = slice(starts[k], starts[k] + w)
-            o_bf = sb("o_bf%d" % k, [P, w * LANES], BF16)
+        o_bf = [sb("o_bf%d" % k, [P, w * LANES], BF16) for k, w in enumerate(PIECES)]
+
+        def weave(k):
+            cols = slice(starts[k], starts[k] + PIECES[k])
             word = U32 if k in SCALAR_WEAVES else I32
-            dst = o_bf[:].bitcast(word).rearrange("p (c u) -> p c u", u=2)
+            dst = o_bf[k][:].bitcast(word).rearrange("p (c u) -> p c u", u=2)
             src = pairs[:].bitcast(word).rearrange("p (u c) -> p u c", u=2)[:, :, cols].rearrange("p u c -> p c u")
             if k in SCALAR_WEAVES:
                 nc.scalar.copy(out=dst, in_=src)
             else:
                 nc.vector.tensor_copy(out=dst, in_=src)
-            nc.vector.quantize_mx(out=o_codes[:, cols].bitcast(E4M3), scales=o_scales[:, cols], in_=o_bf[:])
+
+        weave(0)
+        for k, w in enumerate(PIECES):
+            if k + 1 < len(PIECES):
+                weave(k + 1)
+            cols = slice(starts[k], starts[k] + w)
+            nc.vector.quantize_mx(out=o_codes[:, cols].bitcast(E4M3), scales=o_scales[:, cols], in_=o_bf[k][:])
             if cols.stop in STORE_ENDS:
                 run = slice(max([0] + [e for e in STORE_ENDS if e < cols.stop]), cols.stop)
                 nc.sync.dma_start(out=out_words[:, run], in_=o_codes[:, run].bitcast(I32))

@@ -35,7 +35,6 @@ def tile_attend_gml_pl_cau_kernel(tc, xT, wd, wv, y, cw, rw, offs, out_0, out_1,
             return keep.tile(shape, dtype, name=name, tag=tag or name, align_bytes=64)
 
         offsets = keep.tile([P, N // 16], U16, name="offsets")
-        nc.sync.dma_start(offsets[:], offs)
 
         cw_sb = sb("cw_sb", [P, LANES], F32)
         nc.scalar.dma_start(out=cw_sb[:], in_=cw.rearrange("(p t) o -> p (t o)", t=LANES))
@@ -45,8 +44,12 @@ def tile_attend_gml_pl_cau_kernel(tc, xT, wd, wv, y, cw, rw, offs, out_0, out_1,
         x_plane = [sb("x_plane%d" % j, [P, T], F32) for j in range(LANES)]
         for j in range(LANES):
             nc.sync.dma_start(out=x_plane[j][:], in_=x_rows[:, j, :])
-        wd_raw = sb("wd_raw", [P, LANES, V], F32)
-        nc.sync.dma_start(out=wd_raw[:], in_=wd.rearrange("(p j) v -> p j v", j=LANES))
+            if j == 0:
+                nc.sync.dma_start(offsets[:], offs)
+        wd_rows = wd.rearrange("(p j) v -> p j v", j=LANES)
+        wd_raw = [sb("wd_raw%d" % h, [P, LANES, V // 2], F32) for h in range(2)]
+        for h in range(2):
+            nc.sync.dma_start(out=wd_raw[h][:], in_=wd_rows[:, :, h * (V // 2) : (h + 1) * (V // 2)])
         y_rows = y.rearrange("(p t) i -> p t i", t=LANES)
         y_half = [sb("y_half%d" % h, [P, LANES, N // 2], F32) for h in range(2)]
         for h in range(2):
@@ -64,7 +67,7 @@ def tile_attend_gml_pl_cau_kernel(tc, xT, wd, wv, y, cw, rw, offs, out_0, out_1,
         make_identity(nc, ident[:])
         for j in range(LANES):
             nc.vector.memset(window[j][:], 0.0)
-        rw_spread = psum.tile([P, LANES, P], F32, name="rw_spread", tag="grad3")
+        rw_spread = psum.tile([P, LANES, P], F32, name="rw_spread", tag="spread")
         for j in range(LANES):
             nc.tensor.transpose(rw_spread[:, j, :], rw_cols[:, j : j + 1].to_broadcast([P, P]), ident[:])
         weight = sb("weight", [P, LANES, N], F32)
@@ -76,57 +79,98 @@ def tile_attend_gml_pl_cau_kernel(tc, xT, wd, wv, y, cw, rw, offs, out_0, out_1,
                 scale=cw_sb[:, t : t + 1],
             )
 
+        HALF = N // 2
+        turned = sb("turned", [P, LANES, 2, P], F32)
+        late_weight = []
+        for u in range(2):
+            there = psum.tile([P, 2, 2, P], F32, name="there%d" % u, tag="late_weight%d" % u)
+            for k in range(2):
+                for b in range(2):
+                    nc.tensor.transpose(there[:, k, b, :], weight[:, 2 * u + k, HALF + b * P : HALF + (b + 1) * P], ident[:])
+            nc.scalar.copy(out=turned[:, 2 * u : 2 * u + 2], in_=there[:])
+        for u in range(2):
+            back = psum.tile([P, 2, HALF], F32, name="late_weight%d" % u)
+            for k in range(2):
+                for b in range(2):
+                    nc.tensor.transpose(back[:, k, b * P : (b + 1) * P], turned[:, 2 * u + k, b, :], ident[:])
+            late_weight.append(back)
+
         x_bf = sb("x_bf", [P, N, LANES], BF16)
         for j in range(LANES):
             nc.vector.tensor_copy(out=x_bf[:, :, j], in_=x_plane[j][:].indirect(offsets[:]))
         x_codes = sb("x_codes", [P, N], U32)
         x_scales = sb("x_scales", [P, N], U8)
-        nc.vector.quantize_mx(out=x_codes[:].bitcast(E4M3), scales=x_scales[:], in_=x_bf[:].rearrange("p i j -> p (i j)"))
 
-        wd_dealt = wd_raw[:].rearrange("p j (m t) -> p m j t", t=LANES)
-        wd_codes, wd_scales = [], []
-        for h in range(2):
-            half = sb("wd_bf%d" % h, [P, 2, P, LANES], BF16)
-            if h == 0:
-                nc.vector.tensor_copy(out=half[:].rearrange("p t m j -> p m j t"), in_=wd_dealt[:, :, :, 0:2])
-            else:
-                nc.scalar.copy(out=half[:].rearrange("p t m j -> p m j t"), in_=wd_dealt[:, :, :, 2:4])
-            codes = sb("wd_codes%d" % h, [P, 2 * P], U32)
-            scales = sb("wd_scales%d" % h, [P, 2 * P], U8)
-            nc.vector.quantize_mx(out=codes[:].bitcast(E4M3), scales=scales[:], in_=half[:].rearrange("p t m j -> p (t m j)"))
-            wd_codes.append(codes)
-            wd_scales.append(scales)
+        def quantise_x(h):
+            cols = slice(h * (N // 2), (h + 1) * (N // 2))
+            nc.vector.quantize_mx(
+                out=x_codes[:, cols].bitcast(E4M3), scales=x_scales[:, cols], in_=x_bf[:, cols, :].rearrange("p i j -> p (i j)")
+            )
 
-        HALF = N // 2
+        wd_dealt = [raw[:].rearrange("p j (m t) -> p m j t", t=LANES) for raw in wd_raw]
+        wd_bf = [sb("wd_bf%d" % u, [P, 2, P, LANES], BF16) for u in range(2)]
+        wd_codes = [sb("wd_codes%d" % u, [P, 2 * P], U32) for u in range(2)]
+        wd_scales = [sb("wd_scales%d" % u, [P, 2 * P], U8) for u in range(2)]
+
+        def deal_wd(copy, u, h):
+            rows = slice(h * (P // 2), (h + 1) * (P // 2))
+            copy(out=wd_bf[u][:, :, rows, :].rearrange("p t m j -> p m j t"), in_=wd_dealt[h][:, :, :, 2 * u : 2 * u + 2])
+
+        deal_wd(nc.scalar.copy, 0, 0)
+        deal_wd(nc.scalar.copy, 1, 0)
+        deal_wd(nc.scalar.copy, 1, 1)
+        quantise_x(0)
+        deal_wd(nc.vector.tensor_copy, 0, 1)
+        quantise_x(1)
+        for k in range(2):
+            head = slice(k * P, (k + 1) * P)
+            nc.vector.quantize_mx(
+                out=wd_codes[0][:, head].bitcast(E4M3), scales=wd_scales[0][:, head], in_=wd_bf[0][:, k].rearrange("p m j -> p (m j)")
+            )
+        nc.vector.quantize_mx(out=wd_codes[1][:].bitcast(E4M3), scales=wd_scales[1][:], in_=wd_bf[1][:].rearrange("p t m j -> p (t m j)"))
+
         g_codes = sb("g_codes", [P, N], U32)
         g_scales = sb("g_scales", [P, N], U8)
         nc.vector.memset(g_codes[:, HALF:], 0)
         nc.vector.memset(g_scales[:, HALF:], 0)
+        groups = (((0, 1), (1, 1), (2, 2)), ((0, 2), (2, 2)))
         resid = [sb("q%d" % h, [P, LANES, HALF], F32) for h in range(2)]
         for h in range(2):
             cols = slice(h * HALF, (h + 1) * HALF)
-            for u in range(2):
-                scores = psum.tile([P, 2, HALF], F32, name="scores%d" % (2 * h + u))
-                for k in range(2):
-                    head = slice(k * P, (k + 1) * P)
+            for first, count in groups[h]:
+                scores = psum.tile([P, count, HALF], F32, name="scores%d_%d" % (h, first))
+                for k in range(count):
+                    t = first + k
+                    head = slice((t % 2) * P, (t % 2 + 1) * P)
                     nc.tensor.matmul_mx(
                         out=scores[:, k, :],
-                        lhsT=wd_codes[u][:, head].bitcast(E4M3),
-                        lhsT_scale=wd_scales[u][:, head],
+                        lhsT=wd_codes[t // 2][:, head].bitcast(E4M3),
+                        lhsT_scale=wd_scales[t // 2][:, head],
                         rhs=x_codes[:, cols].bitcast(E4M3),
                         rhs_scale=x_scales[:, cols],
                         start=True,
                         stop=True,
                     )
-                tiles = slice(2 * u, 2 * u + 2)
+                tiles = slice(first, first + count)
                 nc.vector.tensor_tensor(out=resid[h][:, tiles, :], in0=scores[:], in1=y_half[h][:, tiles, :], op=ALU.subtract)
         damp = []
+        weighted = [sb("h%d" % h, [P, LANES, HALF], F32) for h in range(2)]
         for h in range(2):
             q_sq = sb("q_sq%d" % h, [P, LANES, HALF], F32)
             root = sb("root%d" % h, [P, LANES, HALF], F32)
-            for u in range(2):
-                tiles = slice(2 * u, 2 * u + 2)
-                nc.scalar.activation(out=q_sq[:, tiles, :], in_=resid[h][:, tiles, :], func=ACT.Square)
+            for first, count in groups[h]:
+                tiles = slice(first, first + count)
+                if (h, first) != (1, 2):
+                    nc.scalar.activation(out=q_sq[:, tiles, :], in_=resid[h][:, tiles, :], func=ACT.Square)
+            if h == 1:
+                for u in range(2):
+                    tiles = slice(2 * u, 2 * u + 2)
+                    nc.vector.tensor_tensor(out=weighted[1][:, tiles, :], in0=late_weight[u][:], in1=resid[1][:, tiles, :], op=ALU.mult)
+                nc.vector.tensor_tensor(out=q_sq[:, 2:4, :], in0=resid[1][:, 2:4, :], in1=resid[1][:, 2:4, :], op=ALU.mult)
+            else:
+                for u in range(2):
+                    tiles = slice(2 * u, 2 * u + 2)
+                    nc.gpsimd.tensor_tensor(out=weighted[0][:, tiles, :], in0=resid[0][:, tiles, :], in1=weight[:, tiles, :HALF], op=ALU.mult)
             for u in range(2):
                 tiles = slice(2 * u, 2 * u + 2)
                 nc.scalar.activation(out=root[:, tiles, :], in_=q_sq[:, tiles, :], func=ACT.Abs_reciprocal_sqrt, bias=1.0)
@@ -134,12 +178,6 @@ def tile_attend_gml_pl_cau_kernel(tc, xT, wd, wv, y, cw, rw, offs, out_0, out_1,
                 inv = sb("inv%d" % (2 * h + k), [P, LANES, CHUNK], F32)
                 nc.scalar.activation(out=inv[:], in_=root[:, :, k * CHUNK : (k + 1) * CHUNK], func=ACT.Square)
                 damp.append(inv)
-        weighted = []
-        for h in range(2):
-            prod = sb("h%d" % h, [P, LANES, HALF], F32)
-            nc.vector.tensor_tensor(out=prod[:], in0=resid[h][:], in1=weight[:, :, h * HALF : (h + 1) * HALF], op=ALU.mult)
-            weighted.append(prod)
-
         wv_dealt = wv_raw[:].rearrange("p t (m j) -> p m t j", j=LANES)
         wv_bf = []
         wv_codes = [sb("wv_codes%d" % j, [P, P], U32) for j in range(LANES)]
@@ -186,7 +224,7 @@ def tile_attend_gml_pl_cau_kernel(tc, xT, wd, wv, y, cw, rw, offs, out_0, out_1,
             )
             return grad
 
-        early = gradient(0, "scores0")
+        early = gradient(0, "scores0_0")
         form_g(2)
         form_g(3)
         quantise_g(2)
@@ -194,7 +232,9 @@ def tile_attend_gml_pl_cau_kernel(tc, xT, wd, wv, y, cw, rw, offs, out_0, out_1,
         dx_early = sb("dx_early", [P, HALF], F32, tag="inv2")
         nc.scalar.copy(out=dx_early[:], in_=early[:, :HALF])
         half = sb("wv_bf1", [P, 2, P, LANES], BF16, tag="root1")
-        nc.scalar.copy(out=half[:].rearrange("p j m t -> p m t j"), in_=wv_dealt[:, :, :, 2:4])
+        for part in range(2):
+            rows = slice(part * (P // 2), (part + 1) * (P // 2))
+            nc.scalar.copy(out=half[:, :, rows, :].rearrange("p j m t -> p m t j"), in_=wv_dealt[:, rows, :, 2:4])
         wv_bf.append(half)
         quantise_wv(1)
         nc.vector.tensor_copy(out=window[0][:].indirect(offsets[:, : HALF // 16]), in_=dx_early[:])
@@ -202,10 +242,10 @@ def tile_attend_gml_pl_cau_kernel(tc, xT, wd, wv, y, cw, rw, offs, out_0, out_1,
             quantise_wv(j)
 
         starts = [sum(PIECES[:k]) for k in range(len(PIECES))]
-        pairs = sb("pairs", [P, 2 * T * 2], BF16)
+        pairs = sb("pairs", [P, 2 * T * 2], BF16, tag="g_codes")
         out_rows = out_0.rearrange("(p j) t -> p j t", j=LANES)
         for j in range(LANES):
-            grad = gradient(j, "grad%d" % j)
+            grad = gradient(j, ("scores0_1", "scores0_2", "scores1_0", "scores1_2")[j])
             first = HALF if j == 0 else 0
             dx = sb("dx%d" % j, [P, N - first], F32)
             nc.scalar.copy(out=dx[:], in_=grad[:, first:])

@@ -250,7 +250,7 @@ def tile_attend_gml_pl_cau_kernel(tc, xT, wd, wv, y, cw, rw, offs, out_0, out_1,
             dx = sb("dx%d" % j, [P, N - first], F32)
             nc.scalar.copy(out=dx[:], in_=grad[:, first:])
             nc.vector.tensor_copy(out=window[j][:].indirect(offsets[:, first // 16 :]), in_=dx[:])
-            nc.sync.dma_start(out=out_rows[:, j, :], in_=window[j][:])
+            (nc.scalar if j == 2 else nc.sync).dma_start(out=out_rows[:, j, :], in_=window[j][:])
 
         out_words = out_1[0].rearrange("p t l -> p (t l)").bitcast(I32)
         o_scales = sb("o_scales", [P, T], U8)
@@ -259,7 +259,11 @@ def tile_attend_gml_pl_cau_kernel(tc, xT, wd, wv, y, cw, rw, offs, out_0, out_1,
             spans = [(0, T)] if j < LANES - 1 else list(zip(starts, PIECES))
             for first, w in spans:
                 base = (j // 2) * 2 * T + 2 * first + j % 2
-                nc.scalar.copy(out=pairs[:, base : base + 2 * w - 1 : 2], in_=window[j][:, first : first + w])
+                lane = pairs[:, base : base + 2 * w - 1 : 2]
+                if j < 2:
+                    nc.gpsimd.tensor_scalar(out=lane, in0=window[j][:, first : first + w], scalar1=1.0, scalar2=0.0, op0=ALU.mult, op1=ALU.add)
+                else:
+                    nc.scalar.copy(out=lane, in_=window[j][:, first : first + w])
         o_bf = [sb("o_bf%d" % k, [P, w * LANES], BF16) for k, w in enumerate(PIECES)]
 
         def weave(k):

@@ -20,9 +20,10 @@ ALU = mybir.AluOpType
 P = 128
 LANES = 4
 CHUNK = 128
-PIECES = (128, 128, 256, 256, 256, 256, 256, 256, 256)
-SCALAR_WEAVES = (7, 8)
-STORE_ENDS = (512, 1024, 1536, 1792, 2048)
+PIECE = 256
+VECTOR_COLS = 768
+GPSIMD_COLS = 1024
+PAIRED_COLS = 512
 
 
 def tile_attend_gml_pl_cau_kernel(tc, xT, wd, wv, y, cw, rw, offs, out_0, out_1, out_2):
@@ -96,8 +97,13 @@ def tile_attend_gml_pl_cau_kernel(tc, xT, wd, wv, y, cw, rw, offs, out_0, out_1,
             late_weight.append(back)
 
         x_bf = sb("x_bf", [P, N, LANES], BF16)
-        for j in range(LANES):
+        for j in range(LANES - 1):
             nc.vector.tensor_copy(out=x_bf[:, :, j], in_=x_plane[j][:].indirect(offsets[:]))
+        for h in range(2):
+            nc.vector.tensor_copy(
+                out=x_bf[:, h * HALF : (h + 1) * HALF, LANES - 1],
+                in_=x_plane[LANES - 1][:].indirect(offsets[:, h * HALF // 16 : (h + 1) * HALF // 16]),
+            )
         x_codes = sb("x_codes", [P, N], U32)
         x_scales = sb("x_scales", [P, N], U8)
 
@@ -241,8 +247,8 @@ def tile_attend_gml_pl_cau_kernel(tc, xT, wd, wv, y, cw, rw, offs, out_0, out_1,
         for j in range(2, LANES):
             quantise_wv(j)
 
-        starts = [sum(PIECES[:k]) for k in range(len(PIECES))]
-        pairs = sb("pairs", [P, 2 * T * 2], BF16, tag="g_codes")
+        pairs = sb("pairs", [P, 2 * PAIRED_COLS * 2], BF16, tag="g_scales")
+        o_bf = sb("o_bf", [P, T * LANES], BF16, tag="g_codes")
         out_rows = out_0.rearrange("(p j) t -> p j t", j=LANES)
         for j in range(LANES):
             grad = gradient(j, ("scores0_1", "scores0_2", "scores1_0", "scores1_2")[j])
@@ -250,41 +256,60 @@ def tile_attend_gml_pl_cau_kernel(tc, xT, wd, wv, y, cw, rw, offs, out_0, out_1,
             dx = sb("dx%d" % j, [P, N - first], F32)
             nc.scalar.copy(out=dx[:], in_=grad[:, first:])
             nc.vector.tensor_copy(out=window[j][:].indirect(offsets[:, first // 16 :]), in_=dx[:])
-            (nc.scalar if j == 2 else nc.sync).dma_start(out=out_rows[:, j, :], in_=window[j][:])
+            if j != 2:
+                nc.sync.dma_start(out=out_rows[:, j, :], in_=window[j][:])
 
         out_words = out_1[0].rearrange("p t l -> p (t l)").bitcast(I32)
         o_scales = sb("o_scales", [P, T], U8)
         o_codes = sb("o_codes", [P, T], U32)
-        for j in range(LANES):
-            spans = [(0, T)] if j < LANES - 1 else list(zip(starts, PIECES))
-            for first, w in spans:
-                base = (j // 2) * 2 * T + 2 * first + j % 2
-                lane = pairs[:, base : base + 2 * w - 1 : 2]
-                if j < 2:
-                    nc.gpsimd.tensor_scalar(out=lane, in0=window[j][:, first : first + w], scalar1=1.0, scalar2=0.0, op0=ALU.mult, op1=ALU.add)
-                else:
-                    nc.scalar.copy(out=lane, in_=window[j][:, first : first + w])
-        o_bf = [sb("o_bf%d" % k, [P, w * LANES], BF16) for k, w in enumerate(PIECES)]
+        paired = T - PAIRED_COLS
 
-        def weave(k):
-            cols = slice(starts[k], starts[k] + PIECES[k])
-            word = U32 if k in SCALAR_WEAVES else I32
-            dst = o_bf[k][:].bitcast(word).rearrange("p (c u) -> p c u", u=2)
-            src = pairs[:].bitcast(word).rearrange("p (u c) -> p u c", u=2)[:, :, cols].rearrange("p u c -> p c u")
-            if k in SCALAR_WEAVES:
-                nc.scalar.copy(out=dst, in_=src)
-            else:
-                nc.vector.tensor_copy(out=dst, in_=src)
+        def lane(j, first, stop):
+            return o_bf[:, LANES * first + j : LANES * (stop - 1) + j + 1 : LANES]
 
-        weave(0)
-        for k, w in enumerate(PIECES):
-            if k + 1 < len(PIECES):
-                weave(k + 1)
-            cols = slice(starts[k], starts[k] + w)
-            nc.vector.quantize_mx(out=o_codes[:, cols].bitcast(E4M3), scales=o_scales[:, cols], in_=o_bf[k][:])
-            if cols.stop in STORE_ENDS:
-                run = slice(max([0] + [e for e in STORE_ENDS if e < cols.stop]), cols.stop)
-                nc.sync.dma_start(out=out_words[:, run], in_=o_codes[:, run].bitcast(I32))
+        def half_word(j, first, stop):
+            base = (j // 2) * 2 * PAIRED_COLS + j % 2
+            return pairs[:, base + 2 * (first - paired) : base + 2 * (stop - paired) - 1 : 2]
+
+        for j in range(LANES - 1):
+            split = GPSIMD_COLS if j < 2 else VECTOR_COLS
+            if j == 2:
+                nc.scalar.dma_start(out=out_rows[:, j, :], in_=window[j][:])
+            nc.gpsimd.tensor_scalar(out=lane(j, 0, split), in0=window[j][:, :split], scalar1=1.0, scalar2=0.0, op0=ALU.mult, op1=ALU.add)
+            nc.scalar.copy(out=half_word(j, paired, T), in_=window[j][:, paired:])
+            nc.scalar.copy(out=lane(j, split, paired), in_=window[j][:, split:paired])
+        last = LANES - 1
+        one = sb("one", [P, 1], F32)
+        nc.gpsimd.tensor_scalar(out=one[:], in0=lane(2, VECTOR_COLS - 1, VECTOR_COLS), scalar1=1.0, scalar2=1.0, op0=ALU.min, op1=ALU.max)
+        for first in range(paired, T, PIECE):
+            nc.scalar.copy(out=half_word(last, first, first + PIECE), in_=window[last][:, first : first + PIECE])
+        for first in range(VECTOR_COLS, paired, PIECE):
+            nc.scalar.copy(out=lane(last, first, first + PIECE), in_=window[last][:, first : first + PIECE])
+
+        def complete(first):
+            stop = first + PIECE
+            if first < VECTOR_COLS:
+                nc.vector.tensor_scalar(out=lane(last, first, stop), in0=window[last][:, first:stop], scalar1=one[:], scalar2=None, op0=ALU.mult)
+            elif first >= paired:
+                words = pairs[:].bitcast(I32).rearrange("p (u c) -> p u c", u=2)[:, :, first - paired : stop - paired]
+                nc.vector.tensor_copy(
+                    out=o_bf[:, LANES * first : LANES * stop].bitcast(I32).rearrange("p (c u) -> p c u", u=2),
+                    in_=words.rearrange("p u c -> p c u"),
+                )
+
+        order = list(range(0, VECTOR_COLS, PIECE)) + list(range(paired, T, PIECE)) + list(range(VECTOR_COLS, paired, PIECE))
+        runs = ((0, 512), (512, 768), (paired, T), (768, 1280), (1280, paired))
+        complete(order[0])
+        for k, first in enumerate(order):
+            if k + 1 < len(order):
+                complete(order[k + 1])
+            cols = slice(first, first + PIECE)
+            nc.vector.quantize_mx(
+                out=o_codes[:, cols].bitcast(E4M3), scales=o_scales[:, cols], in_=o_bf[:, LANES * first : LANES * cols.stop]
+            )
+            for begin, end in runs:
+                if end == cols.stop:
+                    nc.sync.dma_start(out=out_words[:, begin:end], in_=o_codes[:, begin:end].bitcast(I32))
         for r in range(4):
             queue = nc.sync if r % 2 else nc.scalar
             queue.dma_start(out=out_2[0, r:16:4, :].bitcast(I32), in_=o_scales[r:P:32, :].bitcast(I32))

@@ -19,11 +19,16 @@ ALU = mybir.AluOpType
 
 P = 128
 LANES = 4
+PER_COLUMN = 16
+HALF = N // 2
 CHUNK = 128
+BANK_GROUPS = (((0, 1), (1, 1), (2, 2)), ((0, 2), (2, 2)))
 PIECE = 256
 VECTOR_COLS = 768
-GPSIMD_COLS = 1024
 PAIRED_COLS = 512
+GPSIMD_EXTRA = 256
+WORD_STORE_ENDS = (512, 768, 1280, 1792, 2048)
+SCALE_GROUP = T // 4
 
 
 def tile_attend_gml_pl_cau_kernel(tc, xT, wd, wv, y, cw, rw, offs, out_0, out_1, out_2):
@@ -35,26 +40,28 @@ def tile_attend_gml_pl_cau_kernel(tc, xT, wd, wv, y, cw, rw, offs, out_0, out_1,
         def sb(name, shape, dtype, tag=""):
             return keep.tile(shape, dtype, name=name, tag=tag or name, align_bytes=64)
 
-        offsets = keep.tile([P, N // 16], U16, name="offsets")
+        def entries(first, stop):
+            return offsets[:, first // PER_COLUMN : stop // PER_COLUMN]
 
+        offsets = keep.tile([P, N // PER_COLUMN], U16, name="offsets")
         cw_sb = sb("cw_sb", [P, LANES], F32)
         nc.scalar.dma_start(out=cw_sb[:], in_=cw.rearrange("(p t) o -> p (t o)", t=LANES))
         rw_cols = sb("rw_cols", [P, LANES], F32)
         nc.scalar.dma_start(out=rw_cols[:], in_=rw[0:1, :].rearrange("o (p j) -> p (o j)", j=LANES))
         x_rows = xT.rearrange("(p j) t -> p j t", j=LANES)
         x_plane = [sb("x_plane%d" % j, [P, T], F32) for j in range(LANES)]
-        for j in range(LANES):
+        nc.sync.dma_start(out=x_plane[0][:], in_=x_rows[:, 0, :])
+        nc.sync.dma_start(offsets[:], offs)
+        for j in range(1, LANES):
             nc.sync.dma_start(out=x_plane[j][:], in_=x_rows[:, j, :])
-            if j == 0:
-                nc.sync.dma_start(offsets[:], offs)
         wd_rows = wd.rearrange("(p j) v -> p j v", j=LANES)
-        wd_raw = [sb("wd_raw%d" % h, [P, LANES, V // 2], F32) for h in range(2)]
-        for h in range(2):
-            nc.sync.dma_start(out=wd_raw[h][:], in_=wd_rows[:, :, h * (V // 2) : (h + 1) * (V // 2)])
+        wd_raw = [sb("wd_raw%d" % part, [P, LANES, V // 2], F32) for part in range(2)]
+        for part in range(2):
+            nc.sync.dma_start(out=wd_raw[part][:], in_=wd_rows[:, :, part * (V // 2) : (part + 1) * (V // 2)])
         y_rows = y.rearrange("(p t) i -> p t i", t=LANES)
-        y_half = [sb("y_half%d" % h, [P, LANES, N // 2], F32) for h in range(2)]
+        y_half = [sb("y_half%d" % h, [P, LANES, HALF], F32) for h in range(2)]
         for h in range(2):
-            nc.sync.dma_start(out=y_half[h][:], in_=y_rows[:, :, h * (N // 2) : (h + 1) * (N // 2)])
+            nc.sync.dma_start(out=y_half[h][:], in_=y_rows[:, :, h * HALF : (h + 1) * HALF])
         wv_raw = sb("wv_raw", [P, LANES, D], F32)
         nc.sync.dma_start(out=wv_raw[:], in_=wv.rearrange("(p t) d -> p t d", t=LANES))
 
@@ -68,7 +75,8 @@ def tile_attend_gml_pl_cau_kernel(tc, xT, wd, wv, y, cw, rw, offs, out_0, out_1,
         make_identity(nc, ident[:])
         for j in range(LANES):
             nc.vector.memset(window[j][:], 0.0)
-        rw_spread = psum.tile([P, LANES, P], F32, name="rw_spread", tag="spread")
+
+        rw_spread = psum.tile([P, LANES, P], F32, name="rw_spread")
         for j in range(LANES):
             nc.tensor.transpose(rw_spread[:, j, :], rw_cols[:, j : j + 1].to_broadcast([P, P]), ident[:])
         weight = sb("weight", [P, LANES, N], F32)
@@ -80,7 +88,6 @@ def tile_attend_gml_pl_cau_kernel(tc, xT, wd, wv, y, cw, rw, offs, out_0, out_1,
                 scale=cw_sb[:, t : t + 1],
             )
 
-        HALF = N // 2
         turned = sb("turned", [P, LANES, 2, P], F32)
         late_weight = []
         for u in range(2):
@@ -96,19 +103,19 @@ def tile_attend_gml_pl_cau_kernel(tc, xT, wd, wv, y, cw, rw, offs, out_0, out_1,
                     nc.tensor.transpose(back[:, k, b * P : (b + 1) * P], turned[:, 2 * u + k, b, :], ident[:])
             late_weight.append(back)
 
+        last = LANES - 1
         x_bf = sb("x_bf", [P, N, LANES], BF16)
-        for j in range(LANES - 1):
+        for j in range(last):
             nc.vector.tensor_copy(out=x_bf[:, :, j], in_=x_plane[j][:].indirect(offsets[:]))
         for h in range(2):
             nc.vector.tensor_copy(
-                out=x_bf[:, h * HALF : (h + 1) * HALF, LANES - 1],
-                in_=x_plane[LANES - 1][:].indirect(offsets[:, h * HALF // 16 : (h + 1) * HALF // 16]),
+                out=x_bf[:, h * HALF : (h + 1) * HALF, last], in_=x_plane[last][:].indirect(entries(h * HALF, (h + 1) * HALF))
             )
         x_codes = sb("x_codes", [P, N], U32)
         x_scales = sb("x_scales", [P, N], U8)
 
         def quantise_x(h):
-            cols = slice(h * (N // 2), (h + 1) * (N // 2))
+            cols = slice(h * HALF, (h + 1) * HALF)
             nc.vector.quantize_mx(
                 out=x_codes[:, cols].bitcast(E4M3), scales=x_scales[:, cols], in_=x_bf[:, cols, :].rearrange("p i j -> p (i j)")
             )
@@ -118,9 +125,9 @@ def tile_attend_gml_pl_cau_kernel(tc, xT, wd, wv, y, cw, rw, offs, out_0, out_1,
         wd_codes = [sb("wd_codes%d" % u, [P, 2 * P], U32) for u in range(2)]
         wd_scales = [sb("wd_scales%d" % u, [P, 2 * P], U8) for u in range(2)]
 
-        def deal_wd(copy, u, h):
-            rows = slice(h * (P // 2), (h + 1) * (P // 2))
-            copy(out=wd_bf[u][:, :, rows, :].rearrange("p t m j -> p m j t"), in_=wd_dealt[h][:, :, :, 2 * u : 2 * u + 2])
+        def deal_wd(copy, u, part):
+            ms = slice(part * (P // 2), (part + 1) * (P // 2))
+            copy(out=wd_bf[u][:, :, ms, :].rearrange("p t m j -> p m j t"), in_=wd_dealt[part][:, :, :, 2 * u : 2 * u + 2])
 
         deal_wd(nc.scalar.copy, 0, 0)
         deal_wd(nc.scalar.copy, 1, 0)
@@ -139,14 +146,14 @@ def tile_attend_gml_pl_cau_kernel(tc, xT, wd, wv, y, cw, rw, offs, out_0, out_1,
         g_scales = sb("g_scales", [P, N], U8)
         nc.vector.memset(g_codes[:, HALF:], 0)
         nc.vector.memset(g_scales[:, HALF:], 0)
-        groups = (((0, 1), (1, 1), (2, 2)), ((0, 2), (2, 2)))
-        resid = [sb("q%d" % h, [P, LANES, HALF], F32) for h in range(2)]
+
+        resid = [sb("resid%d" % h, [P, LANES, HALF], F32) for h in range(2)]
         for h in range(2):
             cols = slice(h * HALF, (h + 1) * HALF)
-            for first, count in groups[h]:
-                scores = psum.tile([P, count, HALF], F32, name="scores%d_%d" % (h, first))
+            for tile0, count in BANK_GROUPS[h]:
+                scores = psum.tile([P, count, HALF], F32, name="scores%d_%d" % (h, tile0))
                 for k in range(count):
-                    t = first + k
+                    t = tile0 + k
                     head = slice((t % 2) * P, (t % 2 + 1) * P)
                     nc.tensor.matmul_mx(
                         out=scores[:, k, :],
@@ -157,35 +164,41 @@ def tile_attend_gml_pl_cau_kernel(tc, xT, wd, wv, y, cw, rw, offs, out_0, out_1,
                         start=True,
                         stop=True,
                     )
-                tiles = slice(first, first + count)
+                tiles = slice(tile0, tile0 + count)
                 nc.vector.tensor_tensor(out=resid[h][:, tiles, :], in0=scores[:], in1=y_half[h][:, tiles, :], op=ALU.subtract)
+
+        tile_pairs = [slice(0, 2), slice(2, 4)]
+        weighted = [sb("weighted%d" % h, [P, LANES, HALF], F32) for h in range(2)]
         damp = []
-        weighted = [sb("h%d" % h, [P, LANES, HALF], F32) for h in range(2)]
-        for h in range(2):
-            q_sq = sb("q_sq%d" % h, [P, LANES, HALF], F32)
-            root = sb("root%d" % h, [P, LANES, HALF], F32)
-            for first, count in groups[h]:
-                tiles = slice(first, first + count)
-                if (h, first) != (1, 2):
-                    nc.scalar.activation(out=q_sq[:, tiles, :], in_=resid[h][:, tiles, :], func=ACT.Square)
-            if h == 1:
-                for u in range(2):
-                    tiles = slice(2 * u, 2 * u + 2)
-                    nc.vector.tensor_tensor(out=weighted[1][:, tiles, :], in0=late_weight[u][:], in1=resid[1][:, tiles, :], op=ALU.mult)
-                nc.vector.tensor_tensor(out=q_sq[:, 2:4, :], in0=resid[1][:, 2:4, :], in1=resid[1][:, 2:4, :], op=ALU.mult)
-            else:
-                for u in range(2):
-                    tiles = slice(2 * u, 2 * u + 2)
-                    nc.gpsimd.tensor_tensor(out=weighted[0][:, tiles, :], in0=resid[0][:, tiles, :], in1=weight[:, tiles, :HALF], op=ALU.mult)
-            for u in range(2):
-                tiles = slice(2 * u, 2 * u + 2)
+
+        def square(tiles, q, q_sq):
+            nc.scalar.activation(out=q_sq[:, tiles, :], in_=q[:, tiles, :], func=ACT.Square)
+
+        def dampen(h, q_sq, root):
+            for tiles in tile_pairs:
                 nc.scalar.activation(out=root[:, tiles, :], in_=q_sq[:, tiles, :], func=ACT.Abs_reciprocal_sqrt, bias=1.0)
-            for k in range(2):
+            for k in range(HALF // CHUNK):
                 inv = sb("inv%d" % (2 * h + k), [P, LANES, CHUNK], F32)
                 nc.scalar.activation(out=inv[:], in_=root[:, :, k * CHUNK : (k + 1) * CHUNK], func=ACT.Square)
                 damp.append(inv)
+
+        q_sq0 = sb("q_sq0", [P, LANES, HALF], F32)
+        root0 = sb("root0", [P, LANES, HALF], F32)
+        for tile0, count in BANK_GROUPS[0]:
+            square(slice(tile0, tile0 + count), resid[0], q_sq0)
+        for tiles in tile_pairs:
+            nc.gpsimd.tensor_tensor(out=weighted[0][:, tiles, :], in0=resid[0][:, tiles, :], in1=weight[:, tiles, :HALF], op=ALU.mult)
+        dampen(0, q_sq0, root0)
+        q_sq1 = sb("q_sq1", [P, LANES, HALF], F32)
+        root1 = sb("root1", [P, LANES, HALF], F32)
+        square(tile_pairs[0], resid[1], q_sq1)
+        for u, tiles in enumerate(tile_pairs):
+            nc.vector.tensor_tensor(out=weighted[1][:, tiles, :], in0=late_weight[u][:], in1=resid[1][:, tiles, :], op=ALU.mult)
+        for engine, t in ((nc.vector, 2), (nc.gpsimd, 3)):
+            engine.tensor_tensor(out=q_sq1[:, t : t + 1, :], in0=resid[1][:, t : t + 1, :], in1=resid[1][:, t : t + 1, :], op=ALU.mult)
+        dampen(1, q_sq1, root1)
+
         wv_dealt = wv_raw[:].rearrange("p t (m j) -> p m t j", j=LANES)
-        wv_bf = []
         wv_codes = [sb("wv_codes%d" % j, [P, P], U32) for j in range(LANES)]
         wv_scales = [sb("wv_scales%d" % j, [P, P], U8) for j in range(LANES)]
         g_bf = [sb("g_bf%d" % c, [P, CHUNK, LANES], BF16) for c in range(N // CHUNK)]
@@ -208,15 +221,6 @@ def tile_attend_gml_pl_cau_kernel(tc, xT, wd, wv, y, cw, rw, offs, out_0, out_1,
                 out=wv_codes[j][:].bitcast(E4M3), scales=wv_scales[j][:], in_=wv_bf[j // 2][:, j % 2, :, :].rearrange("p m t -> p (m t)")
             )
 
-        form_g(0)
-        form_g(1)
-        half = sb("wv_bf0", [P, 2, P, LANES], BF16)
-        nc.vector.tensor_copy(out=half[:].rearrange("p j m t -> p m t j"), in_=wv_dealt[:, :, :, 0:2])
-        wv_bf.append(half)
-        quantise_g(0)
-        quantise_g(1)
-        quantise_wv(0)
-
         def gradient(j, bank):
             grad = psum.tile([P, N], F32, name="grad_" + bank, tag=bank)
             nc.tensor.matmul_mx(
@@ -230,6 +234,13 @@ def tile_attend_gml_pl_cau_kernel(tc, xT, wd, wv, y, cw, rw, offs, out_0, out_1,
             )
             return grad
 
+        form_g(0)
+        form_g(1)
+        wv_bf = [sb("wv_bf0", [P, 2, P, LANES], BF16)]
+        nc.vector.tensor_copy(out=wv_bf[0][:].rearrange("p j m t -> p m t j"), in_=wv_dealt[:, :, :, 0:2])
+        quantise_g(0)
+        quantise_g(1)
+        quantise_wv(0)
         early = gradient(0, "scores0_0")
         form_g(2)
         form_g(3)
@@ -237,79 +248,85 @@ def tile_attend_gml_pl_cau_kernel(tc, xT, wd, wv, y, cw, rw, offs, out_0, out_1,
         quantise_g(3)
         dx_early = sb("dx_early", [P, HALF], F32, tag="inv2")
         nc.scalar.copy(out=dx_early[:], in_=early[:, :HALF])
-        half = sb("wv_bf1", [P, 2, P, LANES], BF16, tag="root1")
+        wv_bf.append(sb("wv_bf1", [P, 2, P, LANES], BF16, tag="root1"))
         for part in range(2):
-            rows = slice(part * (P // 2), (part + 1) * (P // 2))
-            nc.scalar.copy(out=half[:, :, rows, :].rearrange("p j m t -> p m t j"), in_=wv_dealt[:, rows, :, 2:4])
-        wv_bf.append(half)
+            ms = slice(part * (P // 2), (part + 1) * (P // 2))
+            nc.scalar.copy(out=wv_bf[1][:, :, ms, :].rearrange("p j m t -> p m t j"), in_=wv_dealt[:, ms, :, 2:4])
         quantise_wv(1)
-        nc.vector.tensor_copy(out=window[0][:].indirect(offsets[:, : HALF // 16]), in_=dx_early[:])
+        nc.vector.tensor_copy(out=window[0][:].indirect(entries(0, HALF)), in_=dx_early[:])
         for j in range(2, LANES):
             quantise_wv(j)
 
         pairs = sb("pairs", [P, 2 * PAIRED_COLS * 2], BF16, tag="g_scales")
         o_bf = sb("o_bf", [P, T * LANES], BF16, tag="g_codes")
         out_rows = out_0.rearrange("(p j) t -> p j t", j=LANES)
-        for j in range(LANES):
-            grad = gradient(j, ("scores0_1", "scores0_2", "scores1_0", "scores1_2")[j])
+        scalar_stored = 2
+        for j, bank in enumerate(("scores0_1", "scores0_2", "scores1_0", "scores1_2")):
+            grad = gradient(j, bank)
             first = HALF if j == 0 else 0
             dx = sb("dx%d" % j, [P, N - first], F32)
             nc.scalar.copy(out=dx[:], in_=grad[:, first:])
-            nc.vector.tensor_copy(out=window[j][:].indirect(offsets[:, first // 16 :]), in_=dx[:])
-            if j != 2:
+            nc.vector.tensor_copy(out=window[j][:].indirect(entries(first, N)), in_=dx[:])
+            if j != scalar_stored:
                 nc.sync.dma_start(out=out_rows[:, j, :], in_=window[j][:])
 
         out_words = out_1[0].rearrange("p t l -> p (t l)").bitcast(I32)
-        o_scales = sb("o_scales", [P, T], U8)
+        o_scales = sb("o_scales", [P, SCALE_GROUP], U8)
         o_codes = sb("o_codes", [P, T], U32)
-        paired = T - PAIRED_COLS
+        paired_end = VECTOR_COLS + PAIRED_COLS
+        pieces = [(first, first + PIECE) for first in range(0, T, PIECE)]
 
         def lane(j, first, stop):
             return o_bf[:, LANES * first + j : LANES * (stop - 1) + j + 1 : LANES]
 
         def half_word(j, first, stop):
             base = (j // 2) * 2 * PAIRED_COLS + j % 2
-            return pairs[:, base + 2 * (first - paired) : base + 2 * (stop - paired) - 1 : 2]
+            return pairs[:, base + 2 * (first - VECTOR_COLS) : base + 2 * (stop - VECTOR_COLS) - 1 : 2]
 
-        for j in range(LANES - 1):
-            split = GPSIMD_COLS if j < 2 else VECTOR_COLS
-            if j == 2:
+        def gpsimd_round(j, first, stop):
+            nc.gpsimd.tensor_scalar(out=lane(j, first, stop), in0=window[j][:, first:stop], scalar1=1.0, scalar2=0.0, op0=ALU.mult, op1=ALU.add)
+
+        for j in range(last):
+            extra = GPSIMD_EXTRA if j < 2 else 0
+            if j == scalar_stored:
                 nc.scalar.dma_start(out=out_rows[:, j, :], in_=window[j][:])
-            nc.gpsimd.tensor_scalar(out=lane(j, 0, split), in0=window[j][:, :split], scalar1=1.0, scalar2=0.0, op0=ALU.mult, op1=ALU.add)
-            nc.scalar.copy(out=half_word(j, paired, T), in_=window[j][:, paired:])
-            nc.scalar.copy(out=lane(j, split, paired), in_=window[j][:, split:paired])
-        last = LANES - 1
+            gpsimd_round(j, 0, VECTOR_COLS)
+            if extra:
+                gpsimd_round(j, paired_end, paired_end + extra)
+            nc.scalar.copy(out=half_word(j, VECTOR_COLS, paired_end), in_=window[j][:, VECTOR_COLS:paired_end])
+            nc.scalar.copy(out=lane(j, paired_end + extra, T), in_=window[j][:, paired_end + extra :])
         one = sb("one", [P, 1], F32)
         nc.gpsimd.tensor_scalar(out=one[:], in0=lane(2, VECTOR_COLS - 1, VECTOR_COLS), scalar1=1.0, scalar2=1.0, op0=ALU.min, op1=ALU.max)
-        for first in range(paired, T, PIECE):
-            nc.scalar.copy(out=half_word(last, first, first + PIECE), in_=window[last][:, first : first + PIECE])
-        for first in range(VECTOR_COLS, paired, PIECE):
-            nc.scalar.copy(out=lane(last, first, first + PIECE), in_=window[last][:, first : first + PIECE])
+        for first, stop in pieces:
+            if first >= VECTOR_COLS:
+                target = half_word if first < paired_end else lane
+                nc.scalar.copy(out=target(last, first, stop), in_=window[last][:, first:stop])
 
-        def complete(first):
-            stop = first + PIECE
+        def complete(first, stop):
             if first < VECTOR_COLS:
                 nc.vector.tensor_scalar(out=lane(last, first, stop), in0=window[last][:, first:stop], scalar1=one[:], scalar2=None, op0=ALU.mult)
-            elif first >= paired:
-                words = pairs[:].bitcast(I32).rearrange("p (u c) -> p u c", u=2)[:, :, first - paired : stop - paired]
+            elif first < paired_end:
+                words = pairs[:].bitcast(I32).rearrange("p (u c) -> p u c", u=2)[:, :, first - VECTOR_COLS : stop - VECTOR_COLS]
                 nc.vector.tensor_copy(
                     out=o_bf[:, LANES * first : LANES * stop].bitcast(I32).rearrange("p (c u) -> p c u", u=2),
                     in_=words.rearrange("p u c -> p c u"),
                 )
 
-        order = list(range(0, VECTOR_COLS, PIECE)) + list(range(paired, T, PIECE)) + list(range(VECTOR_COLS, paired, PIECE))
-        runs = ((0, 512), (512, 768), (paired, T), (768, 1280), (1280, paired))
-        complete(order[0])
-        for k, first in enumerate(order):
-            if k + 1 < len(order):
-                complete(order[k + 1])
-            cols = slice(first, first + PIECE)
+        complete(*pieces[0])
+        stored = 0
+        for k, (first, stop) in enumerate(pieces):
+            if k + 1 < len(pieces):
+                complete(*pieces[k + 1])
+            group, column = divmod(first, SCALE_GROUP)
             nc.vector.quantize_mx(
-                out=o_codes[:, cols].bitcast(E4M3), scales=o_scales[:, cols], in_=o_bf[:, LANES * first : LANES * cols.stop]
+                out=o_codes[:, first:stop].bitcast(E4M3),
+                scales=o_scales[4 * group :, column : column + PIECE],
+                in_=o_bf[:, LANES * first : LANES * stop],
             )
-            for begin, end in runs:
-                if end == cols.stop:
-                    nc.sync.dma_start(out=out_words[:, begin:end], in_=o_codes[:, begin:end].bitcast(I32))
-        for r in range(4):
-            queue = nc.sync if r % 2 else nc.scalar
-            queue.dma_start(out=out_2[0, r:16:4, :].bitcast(I32), in_=o_scales[r:P:32, :].bitcast(I32))
+            if stop in WORD_STORE_ENDS:
+                nc.sync.dma_start(out=out_words[:, stored:stop], in_=o_codes[:, stored:stop].bitcast(I32))
+                stored = stop
+        for quadrant in range(4):
+            queue = nc.sync if quadrant % 2 else nc.scalar
+            rows = out_2[0, 4 * quadrant : 4 * quadrant + 4, :].bitcast(I32).rearrange("r (k c) -> k r c", k=4)
+            queue.dma_start(out=rows, in_=o_scales[32 * quadrant : 32 * quadrant + 16, :].bitcast(I32))

@@ -22,7 +22,7 @@ LANES = 4
 PER_COLUMN = 16
 HALF = N // 2
 CHUNK = 128
-BANK_GROUPS = (((0, 1), (1, 1), (2, 2)), ((0, 2), (2, 2)))
+BANK_GROUPS = (((0, 1), (1, 1), (2, 1), (3, 1)), ((0, 2), (2, 2)))
 PIECE = 256
 VECTOR_COLS = 768
 PAIRED_COLS = 512
@@ -133,14 +133,14 @@ def tile_attend_gml_pl_cau_kernel(tc, xT, wd, wv, y, cw, rw, offs, out_0, out_1,
         deal_wd(nc.scalar.copy, 1, 0)
         deal_wd(nc.scalar.copy, 1, 1)
         quantise_x(0)
-        deal_wd(nc.vector.tensor_copy, 0, 1)
         quantise_x(1)
-        for k in range(2):
+        deal_wd(nc.vector.tensor_copy, 0, 1)
+        for t in range(LANES):
+            u, k = divmod(t, 2)
             head = slice(k * P, (k + 1) * P)
             nc.vector.quantize_mx(
-                out=wd_codes[0][:, head].bitcast(E4M3), scales=wd_scales[0][:, head], in_=wd_bf[0][:, k].rearrange("p m j -> p (m j)")
+                out=wd_codes[u][:, head].bitcast(E4M3), scales=wd_scales[u][:, head], in_=wd_bf[u][:, k].rearrange("p m j -> p (m j)")
             )
-        nc.vector.quantize_mx(out=wd_codes[1][:].bitcast(E4M3), scales=wd_scales[1][:], in_=wd_bf[1][:].rearrange("p t m j -> p (t m j)"))
 
         g_codes = sb("g_codes", [P, N], U32)
         g_scales = sb("g_scales", [P, N], U8)
@@ -151,7 +151,8 @@ def tile_attend_gml_pl_cau_kernel(tc, xT, wd, wv, y, cw, rw, offs, out_0, out_1,
         for h in range(2):
             cols = slice(h * HALF, (h + 1) * HALF)
             for tile0, count in BANK_GROUPS[h]:
-                scores = psum.tile([P, count, HALF], F32, name="scores%d_%d" % (h, tile0))
+                bank = tile0 if h == 0 else tile0 // 2
+                scores = psum.tile([P, count, HALF], F32, name="scores%d_%d" % (h, tile0), tag="bank%d" % bank)
                 for k in range(count):
                     t = tile0 + k
                     head = slice((t % 2) * P, (t % 2 + 1) * P)
@@ -171,32 +172,41 @@ def tile_attend_gml_pl_cau_kernel(tc, xT, wd, wv, y, cw, rw, offs, out_0, out_1,
         weighted = [sb("weighted%d" % h, [P, LANES, HALF], F32) for h in range(2)]
         damp = []
 
-        def square(tiles, q, q_sq):
-            nc.scalar.activation(out=q_sq[:, tiles, :], in_=q[:, tiles, :], func=ACT.Square)
+        chunks = [slice(k * CHUNK, (k + 1) * CHUNK) for k in range(HALF // CHUNK)]
+        whole = slice(0, HALF)
 
-        def dampen(h, q_sq, root):
-            for tiles in tile_pairs:
-                nc.scalar.activation(out=root[:, tiles, :], in_=q_sq[:, tiles, :], func=ACT.Abs_reciprocal_sqrt, bias=1.0)
-            for k in range(HALF // CHUNK):
+        def square(q, q_sq, tiles, cols):
+            nc.scalar.activation(out=q_sq[:, tiles, cols], in_=q[:, tiles, cols], func=ACT.Square)
+
+        def take_root(q_sq, root, tiles, cols):
+            nc.scalar.activation(out=root[:, tiles, cols], in_=q_sq[:, tiles, cols], func=ACT.Abs_reciprocal_sqrt, bias=1.0)
+
+        def dampen(h, root):
+            for k, cols in enumerate(chunks):
                 inv = sb("inv%d" % (2 * h + k), [P, LANES, CHUNK], F32)
-                nc.scalar.activation(out=inv[:], in_=root[:, :, k * CHUNK : (k + 1) * CHUNK], func=ACT.Square)
+                nc.scalar.activation(out=inv[:], in_=root[:, :, cols], func=ACT.Square)
                 damp.append(inv)
 
         q_sq0 = sb("q_sq0", [P, LANES, HALF], F32)
         root0 = sb("root0", [P, LANES, HALF], F32)
-        for tile0, count in BANK_GROUPS[0]:
-            square(slice(tile0, tile0 + count), resid[0], q_sq0)
+        for t in range(LANES):
+            square(resid[0], q_sq0, slice(t, t + 1), whole)
         for tiles in tile_pairs:
             nc.gpsimd.tensor_tensor(out=weighted[0][:, tiles, :], in0=resid[0][:, tiles, :], in1=weight[:, tiles, :HALF], op=ALU.mult)
-        dampen(0, q_sq0, root0)
+        take_root(q_sq0, root0, tile_pairs[0], whole)
+        for cols in chunks:
+            take_root(q_sq0, root0, tile_pairs[1], cols)
+        dampen(0, root0)
         q_sq1 = sb("q_sq1", [P, LANES, HALF], F32)
         root1 = sb("root1", [P, LANES, HALF], F32)
-        square(tile_pairs[0], resid[1], q_sq1)
+        for cols in chunks:
+            square(resid[1], q_sq1, tile_pairs[0], cols)
         for u, tiles in enumerate(tile_pairs):
             nc.vector.tensor_tensor(out=weighted[1][:, tiles, :], in0=late_weight[u][:], in1=resid[1][:, tiles, :], op=ALU.mult)
-        for engine, t in ((nc.vector, 2), (nc.gpsimd, 3)):
-            engine.tensor_tensor(out=q_sq1[:, t : t + 1, :], in0=resid[1][:, t : t + 1, :], in1=resid[1][:, t : t + 1, :], op=ALU.mult)
-        dampen(1, q_sq1, root1)
+        nc.gpsimd.tensor_tensor(out=q_sq1[:, 2:, :], in0=resid[1][:, 2:, :], in1=resid[1][:, 2:, :], op=ALU.mult)
+        for cols in chunks:
+            take_root(q_sq1, root1, slice(0, LANES), cols)
+        dampen(1, root1)
 
         wv_dealt = wv_raw[:].rearrange("p t (m j) -> p m t j", j=LANES)
         wv_codes = [sb("wv_codes%d" % j, [P, P], U32) for j in range(LANES)]
@@ -236,12 +246,12 @@ def tile_attend_gml_pl_cau_kernel(tc, xT, wd, wv, y, cw, rw, offs, out_0, out_1,
 
         form_g(0)
         form_g(1)
-        wv_bf = [sb("wv_bf0", [P, 2, P, LANES], BF16)]
+        wv_bf = [sb("wv_bf0", [P, 2, P, LANES], BF16, tag="inv0")]
         nc.vector.tensor_copy(out=wv_bf[0][:].rearrange("p j m t -> p m t j"), in_=wv_dealt[:, :, :, 0:2])
         quantise_g(0)
         quantise_g(1)
         quantise_wv(0)
-        early = gradient(0, "scores0_0")
+        early = gradient(0, "bank2")
         form_g(2)
         form_g(3)
         quantise_g(2)
@@ -261,7 +271,7 @@ def tile_attend_gml_pl_cau_kernel(tc, xT, wd, wv, y, cw, rw, offs, out_0, out_1,
         o_bf = sb("o_bf", [P, T * LANES], BF16, tag="g_codes")
         out_rows = out_0.rearrange("(p j) t -> p j t", j=LANES)
         scalar_stored = 2
-        for j, bank in enumerate(("scores0_1", "scores0_2", "scores1_0", "scores1_2")):
+        for j, bank in enumerate(("bank3", "bank0", "bank1", "rw_spread")):
             grad = gradient(j, bank)
             first = HALF if j == 0 else 0
             dx = sb("dx%d" % j, [P, N - first], F32)

@@ -24,10 +24,9 @@ HALF = N // 2
 CHUNK = 128
 BANK_GROUPS = (((0, 1), (1, 1), (2, 1), (3, 1)), ((0, 2), (2, 2)))
 PIECE = 256
-VECTOR_COLS = 768
-PAIRED_COLS = 512
-GPSIMD_EXTRA = 256
-WORD_STORE_ENDS = (512, 768, 1280, 1792, 2048)
+SIDE = T // 2
+VECTOR_COLS = 512
+WORD_STORE_ENDS = (768, 1280, 1792, 2048)
 SCALE_GROUP = T // 4
 
 
@@ -144,8 +143,6 @@ def tile_attend_gml_pl_cau_kernel(tc, xT, wd, wv, y, cw, rw, offs, out_0, out_1,
 
         g_codes = sb("g_codes", [P, N], U32)
         g_scales = sb("g_scales", [P, N], U8)
-        nc.vector.memset(g_codes[:, HALF:], 0)
-        nc.vector.memset(g_scales[:, HALF:], 0)
 
         resid = [sb("resid%d" % h, [P, LANES, HALF], F32) for h in range(2)]
         for h in range(2):
@@ -231,18 +228,24 @@ def tile_attend_gml_pl_cau_kernel(tc, xT, wd, wv, y, cw, rw, offs, out_0, out_1,
                 out=wv_codes[j][:].bitcast(E4M3), scales=wv_scales[j][:], in_=wv_bf[j // 2][:, j % 2, :, :].rearrange("p m t -> p (m t)")
             )
 
-        def gradient(j, bank):
-            grad = psum.tile([P, N], F32, name="grad_" + bank, tag=bank)
+        def gradient(j, first, stop, bank):
+            grad = psum.tile([P, stop - first], F32, name="grad_" + bank, tag=bank)
             nc.tensor.matmul_mx(
                 out=grad[:],
                 lhsT=wv_codes[j][:].bitcast(E4M3),
                 lhsT_scale=wv_scales[j][:],
-                rhs=g_codes[:].bitcast(E5M2),
-                rhs_scale=g_scales[:],
+                rhs=g_codes[:, first:stop].bitcast(E5M2),
+                rhs_scale=g_scales[:, first:stop],
                 start=True,
                 stop=True,
             )
             return grad
+
+        def vector_scatter(j, first, stop, values):
+            nc.vector.tensor_copy(out=window[j][:].indirect(entries(first, stop)), in_=values)
+
+        def scalar_scatter(j, first, stop, values):
+            nc.scalar.activation(out=window[j][:].indirect(entries(first, stop)), in_=values, func=ACT.Copy)
 
         form_g(0)
         form_g(1)
@@ -251,82 +254,78 @@ def tile_attend_gml_pl_cau_kernel(tc, xT, wd, wv, y, cw, rw, offs, out_0, out_1,
         quantise_g(0)
         quantise_g(1)
         quantise_wv(0)
-        early = gradient(0, "bank2")
+        early = gradient(0, 0, HALF, "bank2")
         form_g(2)
         form_g(3)
         quantise_g(2)
         quantise_g(3)
         dx_early = sb("dx_early", [P, HALF], F32, tag="inv2")
-        nc.scalar.copy(out=dx_early[:], in_=early[:, :HALF])
+        nc.scalar.copy(out=dx_early[:], in_=early[:])
         wv_bf.append(sb("wv_bf1", [P, 2, P, LANES], BF16, tag="root1"))
         for part in range(2):
             ms = slice(part * (P // 2), (part + 1) * (P // 2))
             nc.scalar.copy(out=wv_bf[1][:, :, ms, :].rearrange("p j m t -> p m t j"), in_=wv_dealt[:, ms, :, 2:4])
         quantise_wv(1)
-        nc.vector.tensor_copy(out=window[0][:].indirect(entries(0, HALF)), in_=dx_early[:])
+        vector_scatter(0, 0, HALF, dx_early[:])
         for j in range(2, LANES):
             quantise_wv(j)
 
-        pairs = sb("pairs", [P, 2 * PAIRED_COLS * 2], BF16, tag="g_scales")
-        o_bf = sb("o_bf", [P, T * LANES], BF16, tag="g_codes")
         out_rows = out_0.rearrange("(p j) t -> p j t", j=LANES)
-        scalar_stored = 2
-        for j, bank in enumerate(("bank3", "bank0", "bank1", "rw_spread")):
-            grad = gradient(j, bank)
-            first = HALF if j == 0 else 0
-            dx = sb("dx%d" % j, [P, N - first], F32)
-            nc.scalar.copy(out=dx[:], in_=grad[:, first:])
-            nc.vector.tensor_copy(out=window[j][:].indirect(entries(first, N)), in_=dx[:])
-            if j != scalar_stored:
-                nc.sync.dma_start(out=out_rows[:, j, :], in_=window[j][:])
+        dx = [sb("dx%d" % j, [P, N - (HALF if j == 0 else 0)], F32) for j in range(LANES)]
+        grad = [gradient(0, HALF, N, "bank3")] + [gradient(j, 0, N, bank) for j, bank in ((1, "bank0"), (2, "bank1"), (3, "rw_spread"))]
+        nc.scalar.copy(out=dx[0][:], in_=grad[0][:])
+        nc.scalar.copy(out=dx[1][:], in_=grad[1][:])
+        scalar_scatter(1, 0, HALF, dx[1][:, :HALF])
+        vector_scatter(0, HALF, N, dx[0][:])
+        nc.sync.dma_start(out=out_rows[:, 0, :], in_=window[0][:])
+        nc.vector.tensor_copy(out=dx[2][:], in_=grad[2][:])
+        nc.scalar.copy(out=dx[3][:], in_=grad[3][:])
+        scalar_scatter(1, HALF, N, dx[1][:, HALF:])
+        vector_scatter(2, 0, N, dx[2][:])
+        scalar_scatter(3, 0, HALF, dx[3][:, :HALF])
+        nc.scalar.dma_start(out=out_rows[:, 1, :], in_=window[1][:])
+        nc.sync.dma_start(out=out_rows[:, 2, :], in_=window[2][:])
+        scalar_scatter(3, HALF, N, dx[3][:, HALF:])
+        nc.scalar.dma_start(out=out_rows[:, 3, :], in_=window[3][:])
+
+        pairs = [sb("pairs0", [P, 2 * SIDE * 2], BF16), sb("pairs1", [P, 2 * SIDE * 2], BF16, tag="dx2")]
+        o_bf = sb("o_bf", [P, T * LANES], BF16)
 
         out_words = out_1[0].rearrange("p t l -> p (t l)").bitcast(I32)
         o_scales = sb("o_scales", [P, SCALE_GROUP], U8)
         o_codes = sb("o_codes", [P, T], U32)
-        paired_end = VECTOR_COLS + PAIRED_COLS
         pieces = [(first, first + PIECE) for first in range(0, T, PIECE)]
 
-        def lane(j, first, stop):
-            return o_bf[:, LANES * first + j : LANES * (stop - 1) + j + 1 : LANES]
-
         def half_word(j, first, stop):
-            base = (j // 2) * 2 * PAIRED_COLS + j % 2
-            return pairs[:, base + 2 * (first - VECTOR_COLS) : base + 2 * (stop - VECTOR_COLS) - 1 : 2]
+            side, column = divmod(first, SIDE)
+            base = (j // 2) * 2 * SIDE + j % 2 + 2 * column
+            return pairs[side][:, base : base + 2 * (stop - first) - 1 : 2]
 
-        def gpsimd_round(j, first, stop):
-            nc.gpsimd.tensor_scalar(out=lane(j, first, stop), in0=window[j][:, first:stop], scalar1=1.0, scalar2=0.0, op0=ALU.mult, op1=ALU.add)
-
-        for j in range(last):
-            extra = GPSIMD_EXTRA if j < 2 else 0
-            if j == scalar_stored:
-                nc.scalar.dma_start(out=out_rows[:, j, :], in_=window[j][:])
-            gpsimd_round(j, 0, VECTOR_COLS)
-            if extra:
-                gpsimd_round(j, paired_end, paired_end + extra)
-            nc.scalar.copy(out=half_word(j, VECTOR_COLS, paired_end), in_=window[j][:, VECTOR_COLS:paired_end])
-            nc.scalar.copy(out=lane(j, paired_end + extra, T), in_=window[j][:, paired_end + extra :])
-        one = sb("one", [P, 1], F32)
-        nc.gpsimd.tensor_scalar(out=one[:], in0=lane(2, VECTOR_COLS - 1, VECTOR_COLS), scalar1=1.0, scalar2=1.0, op0=ALU.min, op1=ALU.max)
+        for j in range(2):
+            nc.gpsimd.tensor_scalar(out=half_word(j, 0, SIDE), in0=window[j][:, :SIDE], scalar1=1.0, scalar2=0.0, op0=ALU.mult, op1=ALU.add)
+        for j in range(2):
+            nc.vector.tensor_copy(out=half_word(j, SIDE, T), in_=window[j][:, SIDE:])
+        nc.vector.tensor_copy(out=half_word(2, 0, VECTOR_COLS), in_=window[2][:, :VECTOR_COLS])
         for first, stop in pieces:
-            if first >= VECTOR_COLS:
-                target = half_word if first < paired_end else lane
-                nc.scalar.copy(out=target(last, first, stop), in_=window[last][:, first:stop])
-
-        def complete(first, stop):
             if first < VECTOR_COLS:
-                nc.vector.tensor_scalar(out=lane(last, first, stop), in0=window[last][:, first:stop], scalar1=one[:], scalar2=None, op0=ALU.mult)
-            elif first < paired_end:
-                words = pairs[:].bitcast(I32).rearrange("p (u c) -> p u c", u=2)[:, :, first - VECTOR_COLS : stop - VECTOR_COLS]
-                nc.vector.tensor_copy(
-                    out=o_bf[:, LANES * first : LANES * stop].bitcast(I32).rearrange("p (c u) -> p c u", u=2),
-                    in_=words.rearrange("p u c -> p c u"),
-                )
+                nc.vector.tensor_copy(out=half_word(last, first, stop), in_=window[last][:, first:stop])
+            else:
+                for j in (2, last):
+                    nc.scalar.copy(out=half_word(j, first, stop), in_=window[j][:, first:stop])
 
-        complete(*pieces[0])
+        def weave(first, stop):
+            side, column = divmod(first, SIDE)
+            words = pairs[side][:].bitcast(I32).rearrange("p (u c) -> p u c", u=2)[:, :, column : column + stop - first]
+            nc.vector.tensor_copy(
+                out=o_bf[:, LANES * first : LANES * stop].bitcast(I32).rearrange("p (c u) -> p c u", u=2),
+                in_=words.rearrange("p u c -> p c u"),
+            )
+
+        weave(*pieces[0])
         stored = 0
         for k, (first, stop) in enumerate(pieces):
             if k + 1 < len(pieces):
-                complete(*pieces[k + 1])
+                weave(*pieces[k + 1])
             group, column = divmod(first, SCALE_GROUP)
             nc.vector.quantize_mx(
                 out=o_codes[:, first:stop].bitcast(E4M3),

@@ -24,8 +24,8 @@ HALF = N // 2
 CHUNK = 128
 BANK_GROUPS = (((0, 1), (1, 1), (2, 1), (3, 1)), ((0, 2), (2, 2)))
 PIECE = 256
-SIDE = T // 2
-VECTOR_COLS = 512
+VECTOR_ROUNDS = 512
+VECTOR_LAYS = 1280
 WORD_STORE_ENDS = (768, 1280, 1792, 2048)
 SCALE_GROUP = T // 4
 
@@ -229,7 +229,7 @@ def tile_attend_gml_pl_cau_kernel(tc, xT, wd, wv, y, cw, rw, offs, out_0, out_1,
             )
 
         def gradient(j, first, stop, bank):
-            grad = psum.tile([P, stop - first], F32, name="grad_" + bank, tag=bank)
+            grad = psum.tile([P, stop - first], F32, name="grad%d_%d" % (j, first), tag=bank)
             nc.tensor.matmul_mx(
                 out=grad[:],
                 lhsT=wv_codes[j][:].bitcast(E4M3),
@@ -261,76 +261,69 @@ def tile_attend_gml_pl_cau_kernel(tc, xT, wd, wv, y, cw, rw, offs, out_0, out_1,
         quantise_g(3)
         dx_early = sb("dx_early", [P, HALF], F32, tag="inv2")
         nc.scalar.copy(out=dx_early[:], in_=early[:])
-        wv_bf.append(sb("wv_bf1", [P, 2, P, LANES], BF16, tag="root1"))
-        for part in range(2):
-            ms = slice(part * (P // 2), (part + 1) * (P // 2))
-            nc.scalar.copy(out=wv_bf[1][:, :, ms, :].rearrange("p j m t -> p m t j"), in_=wv_dealt[:, ms, :, 2:4])
+        scalar_scatter(0, 0, HALF, dx_early[:])
         quantise_wv(1)
-        vector_scatter(0, 0, HALF, dx_early[:])
-        for j in range(2, LANES):
-            quantise_wv(j)
+        wv_bf.append(sb("wv_bf1", [P, 2, P, LANES], BF16, tag="inv3"))
+        nc.vector.tensor_copy(out=wv_bf[1][:].rearrange("p j m t -> p m t j"), in_=wv_dealt[:, :, :, 2:4])
 
         out_rows = out_0.rearrange("(p j) t -> p j t", j=LANES)
         dx = [sb("dx%d" % j, [P, N - (HALF if j == 0 else 0)], F32) for j in range(LANES)]
-        grad = [gradient(0, HALF, N, "bank3")] + [gradient(j, 0, N, bank) for j, bank in ((1, "bank0"), (2, "bank1"), (3, "rw_spread"))]
-        nc.scalar.copy(out=dx[0][:], in_=grad[0][:])
+        grad = [gradient(0, HALF, N, "bank3"), gradient(1, 0, N, "bank0")]
+        nc.vector.tensor_copy(out=dx[0][:], in_=grad[0][:])
         nc.scalar.copy(out=dx[1][:], in_=grad[1][:])
-        scalar_scatter(1, 0, HALF, dx[1][:, :HALF])
+        quantise_wv(2)
         vector_scatter(0, HALF, N, dx[0][:])
         nc.sync.dma_start(out=out_rows[:, 0, :], in_=window[0][:])
+        quantise_wv(3)
+        grad.extend([gradient(2, 0, N, "bank1"), gradient(3, 0, HALF, "rw_spread"), gradient(3, HALF, N, "bank2")])
         nc.vector.tensor_copy(out=dx[2][:], in_=grad[2][:])
-        nc.scalar.copy(out=dx[3][:], in_=grad[3][:])
+        nc.vector.tensor_copy(out=dx[3][:, HALF:], in_=grad[4][:])
+        scalar_scatter(1, 0, HALF, dx[1][:, :HALF])
+        nc.scalar.copy(out=dx[3][:, :HALF], in_=grad[3][:])
         scalar_scatter(1, HALF, N, dx[1][:, HALF:])
+        nc.sync.dma_start(out=out_rows[:, 1, :], in_=window[1][:])
         vector_scatter(2, 0, N, dx[2][:])
-        scalar_scatter(3, 0, HALF, dx[3][:, :HALF])
-        nc.scalar.dma_start(out=out_rows[:, 1, :], in_=window[1][:])
         nc.sync.dma_start(out=out_rows[:, 2, :], in_=window[2][:])
-        scalar_scatter(3, HALF, N, dx[3][:, HALF:])
-        nc.scalar.dma_start(out=out_rows[:, 3, :], in_=window[3][:])
+        for h in range(2):
+            cols = slice(h * HALF, (h + 1) * HALF)
+            scalar_scatter(3, cols.start, cols.stop, dx[3][:, cols])
+        nc.sync.dma_start(out=out_rows[:, 3, :], in_=window[3][:])
 
-        pairs = [sb("pairs0", [P, 2 * SIDE * 2], BF16), sb("pairs1", [P, 2 * SIDE * 2], BF16, tag="dx2")]
-        o_bf = sb("o_bf", [P, T * LANES], BF16)
+        rounded = sb("rounded", [P, LANES, T], BF16)
+        o_bf = sb("o_bf", [P, T, LANES], BF16)
 
         out_words = out_1[0].rearrange("p t l -> p (t l)").bitcast(I32)
         o_scales = sb("o_scales", [P, SCALE_GROUP], U8)
         o_codes = sb("o_codes", [P, T], U32)
         pieces = [(first, first + PIECE) for first in range(0, T, PIECE)]
 
-        def half_word(j, first, stop):
-            side, column = divmod(first, SIDE)
-            base = (j // 2) * 2 * SIDE + j % 2 + 2 * column
-            return pairs[side][:, base : base + 2 * (stop - first) - 1 : 2]
+        for j, stop in enumerate((T, T - PIECE)):
+            nc.gpsimd.tensor_scalar(out=rounded[:, j, :stop], in0=window[j][:, :stop], scalar1=1.0, scalar2=0.0, op0=ALU.mult, op1=ALU.add)
+        nc.scalar.copy(out=rounded[:, 1, T - PIECE :], in_=window[1][:, T - PIECE :])
+        nc.vector.tensor_copy(out=rounded[:, 2, :], in_=window[2][:])
+        nc.vector.tensor_copy(out=rounded[:, last, :VECTOR_ROUNDS], in_=window[last][:, :VECTOR_ROUNDS])
+        for first in range(VECTOR_ROUNDS, T, 2 * PIECE):
+            nc.scalar.copy(out=rounded[:, last, first : first + 2 * PIECE], in_=window[last][:, first : first + 2 * PIECE])
 
-        for j in range(2):
-            nc.gpsimd.tensor_scalar(out=half_word(j, 0, SIDE), in0=window[j][:, :SIDE], scalar1=1.0, scalar2=0.0, op0=ALU.mult, op1=ALU.add)
-        for j in range(2):
-            nc.vector.tensor_copy(out=half_word(j, SIDE, T), in_=window[j][:, SIDE:])
-        nc.vector.tensor_copy(out=half_word(2, 0, VECTOR_COLS), in_=window[2][:, :VECTOR_COLS])
-        for first, stop in pieces:
-            if first < VECTOR_COLS:
-                nc.vector.tensor_copy(out=half_word(last, first, stop), in_=window[last][:, first:stop])
-            else:
-                for j in (2, last):
-                    nc.scalar.copy(out=half_word(j, first, stop), in_=window[j][:, first:stop])
-
-        def weave(first, stop):
-            side, column = divmod(first, SIDE)
-            words = pairs[side][:].bitcast(I32).rearrange("p (u c) -> p u c", u=2)[:, :, column : column + stop - first]
-            nc.vector.tensor_copy(
-                out=o_bf[:, LANES * first : LANES * stop].bitcast(I32).rearrange("p (c u) -> p c u", u=2),
-                in_=words.rearrange("p u c -> p c u"),
+        def lay(copy, first, stop):
+            copy(
+                out=o_bf[:, first:stop, :].rearrange("p (c i) j -> p c j i", i=4),
+                in_=rounded[:, :, first:stop].rearrange("p j (c i) -> p c j i", i=4),
             )
 
-        weave(*pieces[0])
+        for first, stop in pieces:
+            if first >= VECTOR_LAYS:
+                lay(nc.scalar.copy, first, stop)
+        lay(nc.vector.tensor_copy, *pieces[0])
         stored = 0
         for k, (first, stop) in enumerate(pieces):
-            if k + 1 < len(pieces):
-                weave(*pieces[k + 1])
+            if stop < VECTOR_LAYS:
+                lay(nc.vector.tensor_copy, *pieces[k + 1])
             group, column = divmod(first, SCALE_GROUP)
             nc.vector.quantize_mx(
                 out=o_codes[:, first:stop].bitcast(E4M3),
                 scales=o_scales[4 * group :, column : column + PIECE],
-                in_=o_bf[:, LANES * first : LANES * stop],
+                in_=o_bf[:, first:stop, :].rearrange("p c j -> p (c j)"),
             )
             if stop in WORD_STORE_ENDS:
                 nc.sync.dma_start(out=out_words[:, stored:stop], in_=o_codes[:, stored:stop].bitcast(I32))

@@ -26,6 +26,7 @@ BANK_GROUPS = (((0, 1), (1, 1), (2, 1), (3, 1)), ((0, 2), (2, 2)))
 PIECE = 256
 VECTOR_ROUNDS = 512
 VECTOR_LAYS = 1280
+GPSIMD_STOP = 1408
 WORD_STORE_ENDS = (768, 1280, 1792, 2048)
 SCALE_GROUP = T // 4
 
@@ -188,7 +189,7 @@ def tile_attend_gml_pl_cau_kernel(tc, xT, wd, wv, y, cw, rw, offs, out_0, out_1,
         root0 = sb("root0", [P, LANES, HALF], F32)
         for t in range(LANES):
             square(resid[0], q_sq0, slice(t, t + 1), whole)
-        for tiles in tile_pairs:
+        for tiles in (slice(0, 1), slice(1, 2), tile_pairs[1]):
             nc.gpsimd.tensor_tensor(out=weighted[0][:, tiles, :], in0=resid[0][:, tiles, :], in1=weight[:, tiles, :HALF], op=ALU.mult)
         take_root(q_sq0, root0, tile_pairs[0], whole)
         for cols in chunks:
@@ -228,10 +229,9 @@ def tile_attend_gml_pl_cau_kernel(tc, xT, wd, wv, y, cw, rw, offs, out_0, out_1,
                 out=wv_codes[j][:].bitcast(E4M3), scales=wv_scales[j][:], in_=wv_bf[j // 2][:, j % 2, :, :].rearrange("p m t -> p (m t)")
             )
 
-        def gradient(j, first, stop, bank):
-            grad = psum.tile([P, stop - first], F32, name="grad%d_%d" % (j, first), tag=bank)
+        def multiply(out, j, first, stop):
             nc.tensor.matmul_mx(
-                out=grad[:],
+                out=out,
                 lhsT=wv_codes[j][:].bitcast(E4M3),
                 lhsT_scale=wv_scales[j][:],
                 rhs=g_codes[:, first:stop].bitcast(E5M2),
@@ -239,6 +239,10 @@ def tile_attend_gml_pl_cau_kernel(tc, xT, wd, wv, y, cw, rw, offs, out_0, out_1,
                 start=True,
                 stop=True,
             )
+
+        def gradient(j, first, stop, bank):
+            grad = psum.tile([P, stop - first], F32, name="grad%d_%d" % (j, first), tag=bank)
+            multiply(grad[:], j, first, stop)
             return grad
 
         def vector_scatter(j, first, stop, values):
@@ -254,33 +258,38 @@ def tile_attend_gml_pl_cau_kernel(tc, xT, wd, wv, y, cw, rw, offs, out_0, out_1,
         quantise_g(0)
         quantise_g(1)
         quantise_wv(0)
-        early = gradient(0, 0, HALF, "bank2")
+        quantise_wv(1)
+        early = [gradient(0, 0, HALF, "bank2"), gradient(1, 0, HALF, "late_weight0")]
         form_g(2)
         form_g(3)
         quantise_g(2)
         quantise_g(3)
-        dx_early = sb("dx_early", [P, HALF], F32, tag="inv2")
-        nc.scalar.copy(out=dx_early[:], in_=early[:])
-        scalar_scatter(0, 0, HALF, dx_early[:])
-        quantise_wv(1)
+        dx_early = sb("dx_early", [P, 2, HALF], F32, tag="q_sq1")
+        for j in range(2):
+            nc.scalar.copy(out=dx_early[:, j, :], in_=early[j][:])
+        scalar_scatter(0, 0, HALF, dx_early[:, 0, :])
         wv_bf.append(sb("wv_bf1", [P, 2, P, LANES], BF16, tag="inv3"))
         nc.vector.tensor_copy(out=wv_bf[1][:].rearrange("p j m t -> p m t j"), in_=wv_dealt[:, :, :, 2:4])
 
         out_rows = out_0.rearrange("(p j) t -> p j t", j=LANES)
-        dx = [sb("dx%d" % j, [P, N - (HALF if j == 0 else 0)], F32) for j in range(LANES)]
-        grad = [gradient(0, HALF, N, "bank3"), gradient(1, 0, N, "bank0")]
-        nc.vector.tensor_copy(out=dx[0][:], in_=grad[0][:])
-        nc.scalar.copy(out=dx[1][:], in_=grad[1][:])
+        dx = [sb("dx%d" % j, [P, HALF if j < 2 else N], F32) for j in range(LANES)]
+        grad0 = gradient(0, HALF, N, "bank3")
+        nc.vector.tensor_copy(out=dx[0][:], in_=grad0[:])
         quantise_wv(2)
         vector_scatter(0, HALF, N, dx[0][:])
         nc.sync.dma_start(out=out_rows[:, 0, :], in_=window[0][:])
         quantise_wv(3)
-        grad.extend([gradient(2, 0, N, "bank1"), gradient(3, 0, HALF, "rw_spread"), gradient(3, HALF, N, "bank2")])
-        nc.vector.tensor_copy(out=dx[2][:], in_=grad[2][:])
-        nc.vector.tensor_copy(out=dx[3][:, HALF:], in_=grad[4][:])
-        scalar_scatter(1, 0, HALF, dx[1][:, :HALF])
-        nc.scalar.copy(out=dx[3][:, :HALF], in_=grad[3][:])
-        scalar_scatter(1, HALF, N, dx[1][:, HALF:])
+        grad2 = gradient(2, 0, N, "bank1")
+        for_scalar = psum.tile([P, 2, HALF], F32, name="for_scalar", tag="bank0")
+        multiply(for_scalar[:, 0, :], 1, HALF, N)
+        multiply(for_scalar[:, 1, :], 3, 0, HALF)
+        grad3 = gradient(3, HALF, N, "rw_spread")
+        nc.vector.tensor_copy(out=dx[2][:], in_=grad2[:])
+        nc.vector.tensor_copy(out=dx[3][:, HALF:], in_=grad3[:])
+        scalar_scatter(1, 0, HALF, dx_early[:, 1, :])
+        nc.scalar.copy(out=dx[1][:], in_=for_scalar[:, 0, :])
+        nc.scalar.copy(out=dx[3][:, :HALF], in_=for_scalar[:, 1, :])
+        scalar_scatter(1, HALF, N, dx[1][:])
         nc.sync.dma_start(out=out_rows[:, 1, :], in_=window[1][:])
         vector_scatter(2, 0, N, dx[2][:])
         nc.sync.dma_start(out=out_rows[:, 2, :], in_=window[2][:])
@@ -297,11 +306,13 @@ def tile_attend_gml_pl_cau_kernel(tc, xT, wd, wv, y, cw, rw, offs, out_0, out_1,
         o_codes = sb("o_codes", [P, T], U32)
         pieces = [(first, first + PIECE) for first in range(0, T, PIECE)]
 
-        for j, stop in enumerate((T, T - PIECE)):
+        for j, stop in enumerate((T, GPSIMD_STOP)):
             nc.gpsimd.tensor_scalar(out=rounded[:, j, :stop], in0=window[j][:, :stop], scalar1=1.0, scalar2=0.0, op0=ALU.mult, op1=ALU.add)
         nc.scalar.copy(out=rounded[:, 1, T - PIECE :], in_=window[1][:, T - PIECE :])
         nc.vector.tensor_copy(out=rounded[:, 2, :], in_=window[2][:])
-        nc.vector.tensor_copy(out=rounded[:, last, :VECTOR_ROUNDS], in_=window[last][:, :VECTOR_ROUNDS])
+        nc.vector.tensor_copy(out=rounded[:, 1, GPSIMD_STOP : T - PIECE], in_=window[1][:, GPSIMD_STOP : T - PIECE])
+        for first in range(0, VECTOR_ROUNDS, PIECE):
+            nc.vector.tensor_copy(out=rounded[:, last, first : first + PIECE], in_=window[last][:, first : first + PIECE])
         for first in range(VECTOR_ROUNDS, T, 2 * PIECE):
             nc.scalar.copy(out=rounded[:, last, first : first + 2 * PIECE], in_=window[last][:, first : first + 2 * PIECE])
 

@@ -25,7 +25,7 @@ CHUNK = 128
 BANK_GROUPS = (((0, 1), (1, 1), (2, 1), (3, 1)), ((0, 2), (2, 2)))
 PIECE = 256
 VECTOR_ROUNDS = 512
-VECTOR_LAYS = 1280
+VECTOR_LAYS = 1152
 GPSIMD_STOP = 1408
 WORD_STORE_ENDS = (768, 1280, 1792, 2048)
 SCALE_GROUP = T // 4
@@ -189,7 +189,7 @@ def tile_attend_gml_pl_cau_kernel(tc, xT, wd, wv, y, cw, rw, offs, out_0, out_1,
         root0 = sb("root0", [P, LANES, HALF], F32)
         for t in range(LANES):
             square(resid[0], q_sq0, slice(t, t + 1), whole)
-        for tiles in (slice(0, 1), slice(1, 2), tile_pairs[1]):
+        for tiles in tile_pairs:
             nc.gpsimd.tensor_tensor(out=weighted[0][:, tiles, :], in0=resid[0][:, tiles, :], in1=weight[:, tiles, :HALF], op=ALU.mult)
         take_root(q_sq0, root0, tile_pairs[0], whole)
         for cols in chunks:
@@ -201,7 +201,7 @@ def tile_attend_gml_pl_cau_kernel(tc, xT, wd, wv, y, cw, rw, offs, out_0, out_1,
             square(resid[1], q_sq1, tile_pairs[0], cols)
         for u, tiles in enumerate(tile_pairs):
             nc.vector.tensor_tensor(out=weighted[1][:, tiles, :], in0=late_weight[u][:], in1=resid[1][:, tiles, :], op=ALU.mult)
-        nc.gpsimd.tensor_tensor(out=q_sq1[:, 2:, :], in0=resid[1][:, 2:, :], in1=resid[1][:, 2:, :], op=ALU.mult)
+        nc.vector.tensor_tensor(out=q_sq1[:, 2:, :], in0=resid[1][:, 2:, :], in1=resid[1][:, 2:, :], op=ALU.mult)
         for cols in chunks:
             take_root(q_sq1, root1, slice(0, LANES), cols)
         dampen(1, root1)
@@ -323,13 +323,13 @@ def tile_attend_gml_pl_cau_kernel(tc, xT, wd, wv, y, cw, rw, offs, out_0, out_1,
             )
 
         for first, stop in pieces:
-            if first >= VECTOR_LAYS:
-                lay(nc.scalar.copy, first, stop)
+            if stop > VECTOR_LAYS:
+                lay(nc.scalar.copy, max(first, VECTOR_LAYS), stop)
         lay(nc.vector.tensor_copy, *pieces[0])
         stored = 0
         for k, (first, stop) in enumerate(pieces):
             if stop < VECTOR_LAYS:
-                lay(nc.vector.tensor_copy, *pieces[k + 1])
+                lay(nc.vector.tensor_copy, stop, min(stop + PIECE, VECTOR_LAYS))
             group, column = divmod(first, SCALE_GROUP)
             nc.vector.quantize_mx(
                 out=o_codes[:, first:stop].bitcast(E4M3),

@@ -107,18 +107,15 @@ def tile_attend_gml_pl_cau_kernel(tc, xT, wd, wv, y, cw, rw, offs, out_0, out_1,
         x_bf = sb("x_bf", [P, N, LANES], BF16)
         for j in range(last):
             nc.vector.tensor_copy(out=x_bf[:, :, j], in_=x_plane[j][:].indirect(offsets[:]))
-        for h in range(2):
-            nc.vector.tensor_copy(
-                out=x_bf[:, h * HALF : (h + 1) * HALF, last], in_=x_plane[last][:].indirect(entries(h * HALF, (h + 1) * HALF))
-            )
-        x_codes = sb("x_codes", [P, N], U32)
-        x_scales = sb("x_scales", [P, N], U8)
+        nc.vector.tensor_copy(out=x_bf[:, :HALF, last], in_=x_plane[last][:].indirect(entries(0, HALF)))
+        x_rest = sb("x_rest", [P, HALF], BF16)
+        nc.scalar.activation(out=x_rest[:], in_=x_plane[last][:].indirect(entries(HALF, N)), func=ACT.Copy)
+        x_codes = [sb("x_codes0", [P, HALF], U32)]
+        x_scales = [sb("x_scales%d" % h, [P, HALF], U8) for h in range(2)]
 
         def quantise_x(h):
             cols = slice(h * HALF, (h + 1) * HALF)
-            nc.vector.quantize_mx(
-                out=x_codes[:, cols].bitcast(E4M3), scales=x_scales[:, cols], in_=x_bf[:, cols, :].rearrange("p i j -> p (i j)")
-            )
+            nc.vector.quantize_mx(out=x_codes[h][:].bitcast(E4M3), scales=x_scales[h][:], in_=x_bf[:, cols, :].rearrange("p i j -> p (i j)"))
 
         wd_dealt = [raw[:].rearrange("p j (m t) -> p m j t", t=LANES) for raw in wd_raw]
         wd_bf = [sb("wd_bf%d" % u, [P, 2, P, LANES], BF16) for u in range(2)]
@@ -133,7 +130,7 @@ def tile_attend_gml_pl_cau_kernel(tc, xT, wd, wv, y, cw, rw, offs, out_0, out_1,
         deal_wd(nc.scalar.copy, 1, 0)
         deal_wd(nc.scalar.copy, 1, 1)
         quantise_x(0)
-        quantise_x(1)
+        nc.vector.tensor_copy(out=x_bf[:, HALF:, last], in_=x_rest[:])
         deal_wd(nc.vector.tensor_copy, 0, 1)
         for t in range(LANES):
             u, k = divmod(t, 2)
@@ -142,12 +139,14 @@ def tile_attend_gml_pl_cau_kernel(tc, xT, wd, wv, y, cw, rw, offs, out_0, out_1,
                 out=wd_codes[u][:, head].bitcast(E4M3), scales=wd_scales[u][:, head], in_=wd_bf[u][:, k].rearrange("p m j -> p (m j)")
             )
 
+        x_codes.append(sb("x_codes1", [P, HALF], U32, tag="wd_raw1"))
+        quantise_x(1)
+
         g_codes = sb("g_codes", [P, N], U32)
         g_scales = sb("g_scales", [P, N], U8)
 
         resid = [sb("resid%d" % h, [P, LANES, HALF], F32) for h in range(2)]
         for h in range(2):
-            cols = slice(h * HALF, (h + 1) * HALF)
             for tile0, count in BANK_GROUPS[h]:
                 bank = tile0 if h == 0 else tile0 // 2
                 scores = psum.tile([P, count, HALF], F32, name="scores%d_%d" % (h, tile0), tag="bank%d" % bank)
@@ -158,8 +157,8 @@ def tile_attend_gml_pl_cau_kernel(tc, xT, wd, wv, y, cw, rw, offs, out_0, out_1,
                         out=scores[:, k, :],
                         lhsT=wd_codes[t // 2][:, head].bitcast(E4M3),
                         lhsT_scale=wd_scales[t // 2][:, head],
-                        rhs=x_codes[:, cols].bitcast(E4M3),
-                        rhs_scale=x_scales[:, cols],
+                        rhs=x_codes[h][:].bitcast(E4M3),
+                        rhs_scale=x_scales[h][:],
                         start=True,
                         stop=True,
                     )

@@ -24,9 +24,9 @@ HALF = N // 2
 CHUNK = 128
 BANK_GROUPS = (((0, 1), (1, 1), (2, 1), (3, 1)), ((0, 2), (2, 2)))
 PIECE = 256
+TURNED = 6
+LAID = T - TURNED * P
 VECTOR_ROUNDS = 512
-VECTOR_LAYS = 1152
-GPSIMD_STOP = 1408
 WORD_STORE_ENDS = (768, 1280, 1792, 2048)
 SCALE_GROUP = T // 4
 
@@ -274,20 +274,17 @@ def tile_attend_gml_pl_cau_kernel(tc, xT, wd, wv, y, cw, rw, offs, out_0, out_1,
         dx = [sb("dx%d" % j, [P, HALF if j < 2 else N], F32) for j in range(LANES)]
         grad0 = gradient(0, HALF, N, "bank3")
         nc.vector.tensor_copy(out=dx[0][:], in_=grad0[:])
+        grad1 = gradient(1, HALF, N, "bank0")
         quantise_wv(2)
+        quantise_wv(3)
+        nc.vector.tensor_copy(out=dx[1][:], in_=grad1[:])
         vector_scatter(0, HALF, N, dx[0][:])
         nc.sync.dma_start(out=out_rows[:, 0, :], in_=window[0][:])
-        quantise_wv(3)
         grad2 = gradient(2, 0, N, "bank1")
-        for_scalar = psum.tile([P, 2, HALF], F32, name="for_scalar", tag="bank0")
-        multiply(for_scalar[:, 0, :], 1, HALF, N)
-        multiply(for_scalar[:, 1, :], 3, 0, HALF)
-        grad3 = gradient(3, HALF, N, "rw_spread")
+        grad3 = gradient(3, 0, N, "rw_spread")
+        nc.vector.tensor_copy(out=dx[3][:], in_=grad3[:])
         nc.vector.tensor_copy(out=dx[2][:], in_=grad2[:])
-        nc.vector.tensor_copy(out=dx[3][:, HALF:], in_=grad3[:])
         scalar_scatter(1, 0, HALF, dx_early[:, 1, :])
-        nc.scalar.copy(out=dx[1][:], in_=for_scalar[:, 0, :])
-        nc.scalar.copy(out=dx[3][:, :HALF], in_=for_scalar[:, 1, :])
         scalar_scatter(1, HALF, N, dx[1][:])
         nc.sync.dma_start(out=out_rows[:, 1, :], in_=window[1][:])
         vector_scatter(2, 0, N, dx[2][:])
@@ -297,7 +294,7 @@ def tile_attend_gml_pl_cau_kernel(tc, xT, wd, wv, y, cw, rw, offs, out_0, out_1,
             scalar_scatter(3, cols.start, cols.stop, dx[3][:, cols])
         nc.sync.dma_start(out=out_rows[:, 3, :], in_=window[3][:])
 
-        rounded = sb("rounded", [P, LANES, T], BF16)
+        rounded = sb("rounded", [P, LANES, LAID], BF16)
         o_bf = sb("o_bf", [P, T, LANES], BF16)
 
         out_words = out_1[0].rearrange("p t l -> p (t l)").bitcast(I32)
@@ -305,15 +302,53 @@ def tile_attend_gml_pl_cau_kernel(tc, xT, wd, wv, y, cw, rw, offs, out_0, out_1,
         o_codes = sb("o_codes", [P, T], U32)
         pieces = [(first, first + PIECE) for first in range(0, T, PIECE)]
 
-        for j, stop in enumerate((T, GPSIMD_STOP)):
-            nc.gpsimd.tensor_scalar(out=rounded[:, j, :stop], in0=window[j][:, :stop], scalar1=1.0, scalar2=0.0, op0=ALU.mult, op1=ALU.add)
-        nc.scalar.copy(out=rounded[:, 1, T - PIECE :], in_=window[1][:, T - PIECE :])
-        nc.vector.tensor_copy(out=rounded[:, 2, :], in_=window[2][:])
-        nc.vector.tensor_copy(out=rounded[:, 1, GPSIMD_STOP : T - PIECE], in_=window[1][:, GPSIMD_STOP : T - PIECE])
+        free_banks = (("late_weight1", "bank2", "late_weight0"), ("bank3", "bank0", "bank1"))
+        groups = range(TURNED // 2)
+        across = [[psum.tile([P, 2, 2, P], F32, name="across%d_%d" % (u, k), tag=free_banks[u][k]) for k in groups] for u in range(2)]
+        pairs = [[sb("pairs%d_%d" % (u, k), [P, 2, P, 2], BF16) for k in groups] for u in range(2)]
+        for j in range(LANES):
+            for k in groups:
+                for b in range(2):
+                    first = LAID + (2 * k + b) * P
+                    nc.tensor.transpose(across[j // 2][k][:, b, j % 2, :], window[j][:, first : first + P], ident[:])
+
+        def round_across(u, k, blocks):
+            nc.scalar.copy(out=pairs[u][k][:, blocks], in_=across[u][k][:, blocks].rearrange("c b e p -> c b p e"))
+
+        def turn_back(u, k):
+            words = pairs[u][k][:].rearrange("c b p e -> c (b p e)").bitcast(F32)
+            for b in range(2):
+                nc.tensor.transpose(back[k][:, b, u, :], words[:, b * P : (b + 1) * P], ident[:])
+
+        def round_last(first, stop):
+            nc.scalar.copy(out=rounded[:, last, first:stop], in_=window[last][:, first:stop])
+
+        def weave_back(k):
+            cols = slice(LAID + 2 * k * P, LAID + 2 * (k + 1) * P)
+            words = o_bf[:, cols, :].rearrange("p c j -> p (c j)").bitcast(F32)
+            nc.scalar.copy(out=words.rearrange("p (b c u) -> p b c u", b=2, u=2), in_=back[k][:].rearrange("p b u c -> p b c u"))
+
+        for j in range(2):
+            nc.gpsimd.tensor_scalar(out=rounded[:, j, :], in0=window[j][:, :LAID], scalar1=1.0, scalar2=0.0, op0=ALU.mult, op1=ALU.add)
+        nc.vector.tensor_copy(out=rounded[:, 2, :], in_=window[2][:, :LAID])
         for first in range(0, VECTOR_ROUNDS, PIECE):
             nc.vector.tensor_copy(out=rounded[:, last, first : first + PIECE], in_=window[last][:, first : first + PIECE])
-        for first in range(VECTOR_ROUNDS, T, 2 * PIECE):
-            nc.scalar.copy(out=rounded[:, last, first : first + 2 * PIECE], in_=window[last][:, first : first + 2 * PIECE])
+        middle = (VECTOR_ROUNDS + LAID) // 2
+        back = []
+        round_across(0, 0, slice(0, 1))
+        round_last(VECTOR_ROUNDS, middle)
+        round_across(0, 0, slice(1, 2))
+        round_last(middle, LAID)
+        for k in groups:
+            if k > 0:
+                round_across(0, k, slice(0, 2))
+            back.append(psum.tile([P, 2, 2, P], F32, name="back%d" % k, tag=free_banks[0][k]))
+            turn_back(0, k)
+        for k in groups:
+            round_across(1, k, slice(0, 2))
+            turn_back(1, k)
+        for k in groups:
+            weave_back(k)
 
         def lay(copy, first, stop):
             copy(
@@ -321,14 +356,11 @@ def tile_attend_gml_pl_cau_kernel(tc, xT, wd, wv, y, cw, rw, offs, out_0, out_1,
                 in_=rounded[:, :, first:stop].rearrange("p j (c i) -> p c j i", i=4),
             )
 
-        for first, stop in pieces:
-            if stop > VECTOR_LAYS:
-                lay(nc.scalar.copy, max(first, VECTOR_LAYS), stop)
         lay(nc.vector.tensor_copy, *pieces[0])
         stored = 0
         for k, (first, stop) in enumerate(pieces):
-            if stop < VECTOR_LAYS:
-                lay(nc.vector.tensor_copy, stop, min(stop + PIECE, VECTOR_LAYS))
+            if stop < LAID:
+                lay(nc.vector.tensor_copy, stop, min(stop + PIECE, LAID))
             group, column = divmod(first, SCALE_GROUP)
             nc.vector.quantize_mx(
                 out=o_codes[:, first:stop].bitcast(E4M3),

@@ -26,7 +26,7 @@ BANK_GROUPS = (((0, 1), (1, 1), (2, 1), (3, 1)), ((0, 2), (2, 2)))
 PIECE = 256
 TURNED = 6
 LAID = T - TURNED * P
-VECTOR_ROUNDS = 512
+VECTOR_ROUNDS = 256
 WORD_STORE_ENDS = (768, 1280, 1792, 2048)
 SCALE_GROUP = T // 4
 
@@ -300,7 +300,7 @@ def tile_attend_gml_pl_cau_kernel(tc, xT, wd, wv, y, cw, rw, offs, out_0, out_1,
         out_words = out_1[0].rearrange("p t l -> p (t l)").bitcast(I32)
         o_scales = sb("o_scales", [P, SCALE_GROUP], U8)
         o_codes = sb("o_codes", [P, T], U32)
-        pieces = [(first, first + PIECE) for first in range(0, T, PIECE)]
+        pieces = [(first, first + PIECE) for first in range(0, T - PIECE, PIECE)] + [(T - PIECE, T - P), (T - P, T)]
 
         free_banks = (("late_weight1", "bank2", "late_weight0"), ("bank3", "bank0", "bank1"))
         groups = range(TURNED // 2)
@@ -323,10 +323,10 @@ def tile_attend_gml_pl_cau_kernel(tc, xT, wd, wv, y, cw, rw, offs, out_0, out_1,
         def round_last(first, stop):
             nc.scalar.copy(out=rounded[:, last, first:stop], in_=window[last][:, first:stop])
 
-        def weave_back(k):
-            cols = slice(LAID + 2 * k * P, LAID + 2 * (k + 1) * P)
+        def weave_back(k, blocks):
+            cols = slice(LAID + (2 * k + blocks.start) * P, LAID + (2 * k + blocks.stop) * P)
             words = o_bf[:, cols, :].rearrange("p c j -> p (c j)").bitcast(F32)
-            nc.scalar.copy(out=words.rearrange("p (b c u) -> p b c u", b=2, u=2), in_=back[k][:].rearrange("p b u c -> p b c u"))
+            nc.scalar.copy(out=words.rearrange("p (b c u) -> p b c u", c=P, u=2), in_=back[k][:, blocks].rearrange("p b u c -> p b c u"))
 
         for j in range(2):
             nc.gpsimd.tensor_scalar(out=rounded[:, j, :], in0=window[j][:, :LAID], scalar1=1.0, scalar2=0.0, op0=ALU.mult, op1=ALU.add)
@@ -347,8 +347,10 @@ def tile_attend_gml_pl_cau_kernel(tc, xT, wd, wv, y, cw, rw, offs, out_0, out_1,
         for k in groups:
             round_across(1, k, slice(0, 2))
             turn_back(1, k)
-        for k in groups:
-            weave_back(k)
+        for k in groups[:-1]:
+            weave_back(k, slice(0, 2))
+        for b in range(2):
+            weave_back(groups[-1], slice(b, b + 1))
 
         def lay(copy, first, stop):
             copy(
@@ -364,7 +366,7 @@ def tile_attend_gml_pl_cau_kernel(tc, xT, wd, wv, y, cw, rw, offs, out_0, out_1,
             group, column = divmod(first, SCALE_GROUP)
             nc.vector.quantize_mx(
                 out=o_codes[:, first:stop].bitcast(E4M3),
-                scales=o_scales[4 * group :, column : column + PIECE],
+                scales=o_scales[4 * group :, column : column + stop - first],
                 in_=o_bf[:, first:stop, :].rearrange("p c j -> p (c j)"),
             )
             if stop in WORD_STORE_ENDS:

from contextlib import ExitStack

import concourse.mybir as mybir
from concourse.masks import make_identity

N, T, D, V = 512, 2048, 512, 512
FLOPS = 2 * 2 * N * D * V

F32 = mybir.dt.float32
BF16 = mybir.dt.bfloat16
I32 = mybir.dt.int32
U32 = mybir.dt.uint32
U16 = mybir.dt.uint16
U8 = mybir.dt.uint8
E4M3 = mybir.dt.float8_e4m3fn_x4
E5M2 = mybir.dt.float8_e5m2_x4
ACT = mybir.ActivationFunctionType
ALU = mybir.AluOpType

P = 128
LANES = 4
PER_COLUMN = 16
HALF = N // 2
CHUNK = 128
BANK_GROUPS = (((0, 1), (1, 1), (2, 1), (3, 1)), ((0, 2), (2, 2)))
PIECE = 256
TURNED = 6
LAID = T - TURNED * P
VECTOR_ROUNDS = 256
WORD_STORE_ENDS = (768, 1280, 1792, 2048)
SCALE_GROUP = T // 4


def tile_attend_gml_pl_cau_kernel(tc, xT, wd, wv, y, cw, rw, offs, out_0, out_1, out_2):
    nc = tc.nc
    with ExitStack() as ctx:
        keep = ctx.enter_context(tc.tile_pool(name="keep", bufs=1))
        psum = ctx.enter_context(tc.psum_pool(name="psum", bufs=1))

        def sb(name, shape, dtype, tag=""):
            return keep.tile(shape, dtype, name=name, tag=tag or name, align_bytes=64)

        def entries(first, stop):
            return offsets[:, first // PER_COLUMN : stop // PER_COLUMN]

        offsets = keep.tile([P, N // PER_COLUMN], U16, name="offsets")
        cw_sb = sb("cw_sb", [P, LANES], F32)
        nc.scalar.dma_start(out=cw_sb[:], in_=cw.rearrange("(p t) o -> p (t o)", t=LANES))
        rw_cols = sb("rw_cols", [P, LANES], F32)
        nc.scalar.dma_start(out=rw_cols[:], in_=rw[0:1, :].rearrange("o (p j) -> p (o j)", j=LANES))
        x_rows = xT.rearrange("(p j) t -> p j t", j=LANES)
        x_plane = [sb("x_plane%d" % j, [P, T], F32) for j in range(LANES)]
        nc.sync.dma_start(out=x_plane[0][:], in_=x_rows[:, 0, :])
        nc.sync.dma_start(offsets[:], offs)
        for j in range(1, LANES):
            nc.sync.dma_start(out=x_plane[j][:], in_=x_rows[:, j, :])
        wd_rows = wd.rearrange("(p j) v -> p j v", j=LANES)
        wd_raw = [sb("wd_raw%d" % part, [P, LANES, V // 2], F32) for part in range(2)]
        for part in range(2):
            nc.sync.dma_start(out=wd_raw[part][:], in_=wd_rows[:, :, part * (V // 2) : (part + 1) * (V // 2)])
        y_rows = y.rearrange("(p t) i -> p t i", t=LANES)
        y_half = [sb("y_half%d" % h, [P, LANES, HALF], F32) for h in range(2)]
        for h in range(2):
            nc.sync.dma_start(out=y_half[h][:], in_=y_rows[:, :, h * HALF : (h + 1) * HALF])
        wv_raw = sb("wv_raw", [P, LANES, D], F32)
        nc.sync.dma_start(out=wv_raw[:], in_=wv.rearrange("(p t) d -> p t d", t=LANES))

        warm_in = sb("warm_in", [P, 1], F32)
        warm_out = sb("warm_out", [P, 1], F32)
        nc.vector.memset(warm_in[:], 1.0)
        nc.scalar.activation(out=warm_out[:], in_=warm_in[:], func=ACT.Abs_reciprocal_sqrt)

        window = [sb("window%d" % j, [P, T], F32) for j in range(LANES)]
        ident = sb("ident", [P, P], F32)
        make_identity(nc, ident[:])
        for j in range(LANES):
            nc.vector.memset(window[j][:], 0.0)

        rw_spread = psum.tile([P, LANES, P], F32, name="rw_spread")
        for j in range(LANES):
            nc.tensor.transpose(rw_spread[:, j, :], rw_cols[:, j : j + 1].to_broadcast([P, P]), ident[:])
        weight = sb("weight", [P, LANES, N], F32)
        for t in range(LANES):
            nc.scalar.activation(
                out=weight[:, t, :].rearrange("p (n j) -> p n j", j=LANES),
                in_=rw_spread[:].rearrange("p j n -> p n j"),
                func=ACT.Copy,
                scale=cw_sb[:, t : t + 1],
            )

        turned = sb("turned", [P, LANES, 2, P], F32)
        late_weight = []
        for u in range(2):
            there = psum.tile([P, 2, 2, P], F32, name="there%d" % u, tag="late_weight%d" % u)
            for k in range(2):
                for b in range(2):
                    nc.tensor.transpose(there[:, k, b, :], weight[:, 2 * u + k, HALF + b * P : HALF + (b + 1) * P], ident[:])
            nc.scalar.copy(out=turned[:, 2 * u : 2 * u + 2], in_=there[:])
        for u in range(2):
            back = psum.tile([P, 2, HALF], F32, name="late_weight%d" % u)
            for k in range(2):
                for b in range(2):
                    nc.tensor.transpose(back[:, k, b * P : (b + 1) * P], turned[:, 2 * u + k, b, :], ident[:])
            late_weight.append(back)

        last = LANES - 1
        x_bf = sb("x_bf", [P, N, LANES], BF16)
        for j in range(last):
            nc.vector.tensor_copy(out=x_bf[:, :, j], in_=x_plane[j][:].indirect(offsets[:]))
        nc.vector.tensor_copy(out=x_bf[:, :HALF, last], in_=x_plane[last][:].indirect(entries(0, HALF)))
        x_rest = sb("x_rest", [P, HALF], BF16)
        nc.scalar.activation(out=x_rest[:], in_=x_plane[last][:].indirect(entries(HALF, N)), func=ACT.Copy)
        x_codes = [sb("x_codes0", [P, HALF], U32)]
        x_scales = [sb("x_scales%d" % h, [P, HALF], U8) for h in range(2)]

        def quantise_x(h):
            cols = slice(h * HALF, (h + 1) * HALF)
            nc.vector.quantize_mx(out=x_codes[h][:].bitcast(E4M3), scales=x_scales[h][:], in_=x_bf[:, cols, :].rearrange("p i j -> p (i j)"))

        wd_dealt = [raw[:].rearrange("p j (m t) -> p m j t", t=LANES) for raw in wd_raw]
        wd_bf = [sb("wd_bf%d" % u, [P, 2, P, LANES], BF16) for u in range(2)]
        wd_codes = [sb("wd_codes%d" % u, [P, 2 * P], U32) for u in range(2)]
        wd_scales = [sb("wd_scales%d" % u, [P, 2 * P], U8) for u in range(2)]

        def deal_wd(copy, u, part):
            ms = slice(part * (P // 2), (part + 1) * (P // 2))
            copy(out=wd_bf[u][:, :, ms, :].rearrange("p t m j -> p m j t"), in_=wd_dealt[part][:, :, :, 2 * u : 2 * u + 2])

        deal_wd(nc.scalar.copy, 0, 0)
        deal_wd(nc.scalar.copy, 1, 0)
        deal_wd(nc.scalar.copy, 1, 1)
        quantise_x(0)
        nc.vector.tensor_copy(out=x_bf[:, HALF:, last], in_=x_rest[:])
        deal_wd(nc.vector.tensor_copy, 0, 1)
        for t in range(LANES):
            u, k = divmod(t, 2)
            head = slice(k * P, (k + 1) * P)
            nc.vector.quantize_mx(
                out=wd_codes[u][:, head].bitcast(E4M3), scales=wd_scales[u][:, head], in_=wd_bf[u][:, k].rearrange("p m j -> p (m j)")
            )

        x_codes.append(sb("x_codes1", [P, HALF], U32, tag="wd_raw1"))
        quantise_x(1)

        g_codes = sb("g_codes", [P, N], U32)
        g_scales = sb("g_scales", [P, N], U8)

        resid = [sb("resid%d" % h, [P, LANES, HALF], F32) for h in range(2)]
        for h in range(2):
            for tile0, count in BANK_GROUPS[h]:
                bank = tile0 if h == 0 else tile0 // 2
                scores = psum.tile([P, count, HALF], F32, name="scores%d_%d" % (h, tile0), tag="bank%d" % bank)
                for k in range(count):
                    t = tile0 + k
                    head = slice((t % 2) * P, (t % 2 + 1) * P)
                    nc.tensor.matmul_mx(
                        out=scores[:, k, :],
                        lhsT=wd_codes[t // 2][:, head].bitcast(E4M3),
                        lhsT_scale=wd_scales[t // 2][:, head],
                        rhs=x_codes[h][:].bitcast(E4M3),
                        rhs_scale=x_scales[h][:],
                        start=True,
                        stop=True,
                    )
                tiles = slice(tile0, tile0 + count)
                nc.vector.tensor_tensor(out=resid[h][:, tiles, :], in0=scores[:], in1=y_half[h][:, tiles, :], op=ALU.subtract)

        tile_pairs = [slice(0, 2), slice(2, 4)]
        weighted = [sb("weighted%d" % h, [P, LANES, HALF], F32) for h in range(2)]
        damp = []

        chunks = [slice(k * CHUNK, (k + 1) * CHUNK) for k in range(HALF // CHUNK)]
        whole = slice(0, HALF)

        def square(q, q_sq, tiles, cols):
            nc.scalar.activation(out=q_sq[:, tiles, cols], in_=q[:, tiles, cols], func=ACT.Square)

        def take_root(q_sq, root, tiles, cols):
            nc.scalar.activation(out=root[:, tiles, cols], in_=q_sq[:, tiles, cols], func=ACT.Abs_reciprocal_sqrt, bias=1.0)

        def dampen(h, root):
            for k, cols in enumerate(chunks):
                inv = sb("inv%d" % (2 * h + k), [P, LANES, CHUNK], F32)
                nc.scalar.activation(out=inv[:], in_=root[:, :, cols], func=ACT.Square)
                damp.append(inv)

        q_sq0 = sb("q_sq0", [P, LANES, HALF], F32)
        root0 = sb("root0", [P, LANES, HALF], F32)
        for t in range(LANES):
            square(resid[0], q_sq0, slice(t, t + 1), whole)
        for tiles in tile_pairs:
            nc.gpsimd.tensor_tensor(out=weighted[0][:, tiles, :], in0=resid[0][:, tiles, :], in1=weight[:, tiles, :HALF], op=ALU.mult)
        take_root(q_sq0, root0, tile_pairs[0], whole)
        for cols in chunks:
            take_root(q_sq0, root0, tile_pairs[1], cols)
        dampen(0, root0)
        q_sq1 = sb("q_sq1", [P, LANES, HALF], F32)
        root1 = sb("root1", [P, LANES, HALF], F32)
        for cols in chunks:
            square(resid[1], q_sq1, tile_pairs[0], cols)
        for u, tiles in enumerate(tile_pairs):
            nc.vector.tensor_tensor(out=weighted[1][:, tiles, :], in0=late_weight[u][:], in1=resid[1][:, tiles, :], op=ALU.mult)
        nc.vector.tensor_tensor(out=q_sq1[:, 2:, :], in0=resid[1][:, 2:, :], in1=resid[1][:, 2:, :], op=ALU.mult)
        for cols in chunks:
            take_root(q_sq1, root1, slice(0, LANES), cols)
        dampen(1, root1)

        wv_dealt = wv_raw[:].rearrange("p t (m j) -> p m t j", j=LANES)
        wv_codes = [sb("wv_codes%d" % j, [P, P], U32) for j in range(LANES)]
        wv_scales = [sb("wv_scales%d" % j, [P, P], U8) for j in range(LANES)]
        g_bf = [sb("g_bf%d" % c, [P, CHUNK, LANES], BF16) for c in range(N // CHUNK)]

        def form_g(c):
            inner = slice((c % 2) * CHUNK, (c % 2 + 1) * CHUNK)
            nc.vector.tensor_tensor(
                out=g_bf[c][:].rearrange("p (c i) t -> p c t i", i=4),
                in0=weighted[c // 2][:, :, inner].rearrange("p t (c i) -> p c t i", i=4),
                in1=damp[c][:].rearrange("p t (c i) -> p c t i", i=4),
                op=ALU.mult,
            )

        def quantise_g(c):
            cols = slice(c * CHUNK, (c + 1) * CHUNK)
            nc.vector.quantize_mx(out=g_codes[:, cols].bitcast(E5M2), scales=g_scales[:, cols], in_=g_bf[c][:].rearrange("p i t -> p (i t)"))

        def quantise_wv(j):
            nc.vector.quantize_mx(
                out=wv_codes[j][:].bitcast(E4M3), scales=wv_scales[j][:], in_=wv_bf[j // 2][:, j % 2, :, :].rearrange("p m t -> p (m t)")
            )

        def multiply(out, j, first, stop):
            nc.tensor.matmul_mx(
                out=out,
                lhsT=wv_codes[j][:].bitcast(E4M3),
                lhsT_scale=wv_scales[j][:],
                rhs=g_codes[:, first:stop].bitcast(E5M2),
                rhs_scale=g_scales[:, first:stop],
                start=True,
                stop=True,
            )

        def gradient(j, first, stop, bank):
            grad = psum.tile([P, stop - first], F32, name="grad%d_%d" % (j, first), tag=bank)
            multiply(grad[:], j, first, stop)
            return grad

        def vector_scatter(j, first, stop, values):
            nc.vector.tensor_copy(out=window[j][:].indirect(entries(first, stop)), in_=values)

        def scalar_scatter(j, first, stop, values):
            nc.scalar.activation(out=window[j][:].indirect(entries(first, stop)), in_=values, func=ACT.Copy)

        form_g(0)
        form_g(1)
        wv_bf = [sb("wv_bf0", [P, 2, P, LANES], BF16, tag="inv0")]
        nc.vector.tensor_copy(out=wv_bf[0][:].rearrange("p j m t -> p m t j"), in_=wv_dealt[:, :, :, 0:2])
        quantise_g(0)
        quantise_g(1)
        quantise_wv(0)
        quantise_wv(1)
        early = [gradient(0, 0, HALF, "bank2"), gradient(1, 0, HALF, "late_weight0")]
        form_g(2)
        form_g(3)
        quantise_g(2)
        quantise_g(3)
        dx_early = sb("dx_early", [P, 2, HALF], F32, tag="q_sq1")
        for j in range(2):
            nc.scalar.copy(out=dx_early[:, j, :], in_=early[j][:])
        scalar_scatter(0, 0, HALF, dx_early[:, 0, :])
        wv_bf.append(sb("wv_bf1", [P, 2, P, LANES], BF16, tag="inv3"))
        nc.vector.tensor_copy(out=wv_bf[1][:].rearrange("p j m t -> p m t j"), in_=wv_dealt[:, :, :, 2:4])

        out_rows = out_0.rearrange("(p j) t -> p j t", j=LANES)
        dx = [sb("dx%d" % j, [P, HALF if j < 2 else N], F32) for j in range(LANES)]
        grad0 = gradient(0, HALF, N, "bank3")
        nc.vector.tensor_copy(out=dx[0][:], in_=grad0[:])
        grad1 = gradient(1, HALF, N, "bank0")
        quantise_wv(2)
        quantise_wv(3)
        nc.vector.tensor_copy(out=dx[1][:], in_=grad1[:])
        vector_scatter(0, HALF, N, dx[0][:])
        nc.sync.dma_start(out=out_rows[:, 0, :], in_=window[0][:])
        grad2 = gradient(2, 0, N, "bank1")
        grad3 = gradient(3, 0, N, "rw_spread")
        nc.vector.tensor_copy(out=dx[3][:], in_=grad3[:])
        nc.vector.tensor_copy(out=dx[2][:], in_=grad2[:])
        scalar_scatter(1, 0, HALF, dx_early[:, 1, :])
        scalar_scatter(1, HALF, N, dx[1][:])
        nc.sync.dma_start(out=out_rows[:, 1, :], in_=window[1][:])
        vector_scatter(2, 0, N, dx[2][:])
        nc.sync.dma_start(out=out_rows[:, 2, :], in_=window[2][:])
        for h in range(2):
            cols = slice(h * HALF, (h + 1) * HALF)
            scalar_scatter(3, cols.start, cols.stop, dx[3][:, cols])
        nc.sync.dma_start(out=out_rows[:, 3, :], in_=window[3][:])

        rounded = sb("rounded", [P, LANES, LAID], BF16)
        o_bf = sb("o_bf", [P, T, LANES], BF16)

        out_words = out_1[0].rearrange("p t l -> p (t l)").bitcast(I32)
        o_scales = sb("o_scales", [P, SCALE_GROUP], U8)
        o_codes = sb("o_codes", [P, T], U32)
        pieces = [(first, first + PIECE) for first in range(0, T - PIECE, PIECE)] + [(T - PIECE, T - P), (T - P, T)]

        free_banks = (("late_weight1", "bank2", "late_weight0"), ("bank3", "bank0", "bank1"))
        groups = range(TURNED // 2)
        across = [[psum.tile([P, 2, 2, P], F32, name="across%d_%d" % (u, k), tag=free_banks[u][k]) for k in groups] for u in range(2)]
        pairs = [[sb("pairs%d_%d" % (u, k), [P, 2, P, 2], BF16) for k in groups] for u in range(2)]
        for j in range(LANES):
            for k in groups:
                for b in range(2):
                    first = LAID + (2 * k + b) * P
                    nc.tensor.transpose(across[j // 2][k][:, b, j % 2, :], window[j][:, first : first + P], ident[:])

        def round_across(u, k, blocks):
            nc.scalar.copy(out=pairs[u][k][:, blocks], in_=across[u][k][:, blocks].rearrange("c b e p -> c b p e"))

        def turn_back(u, k):
            words = pairs[u][k][:].rearrange("c b p e -> c (b p e)").bitcast(F32)
            for b in range(2):
                nc.tensor.transpose(back[k][:, b, u, :], words[:, b * P : (b + 1) * P], ident[:])

        def round_last(first, stop):
            nc.scalar.copy(out=rounded[:, last, first:stop], in_=window[last][:, first:stop])

        def weave_back(k, blocks):
            cols = slice(LAID + (2 * k + blocks.start) * P, LAID + (2 * k + blocks.stop) * P)
            words = o_bf[:, cols, :].rearrange("p c j -> p (c j)").bitcast(F32)
            nc.scalar.copy(out=words.rearrange("p (b c u) -> p b c u", c=P, u=2), in_=back[k][:, blocks].rearrange("p b u c -> p b c u"))

        for j in range(2):
            nc.gpsimd.tensor_scalar(out=rounded[:, j, :], in0=window[j][:, :LAID], scalar1=1.0, scalar2=0.0, op0=ALU.mult, op1=ALU.add)
        nc.vector.tensor_copy(out=rounded[:, 2, :], in_=window[2][:, :LAID])
        for first in range(0, VECTOR_ROUNDS, PIECE):
            nc.vector.tensor_copy(out=rounded[:, last, first : first + PIECE], in_=window[last][:, first : first + PIECE])
        middle = (VECTOR_ROUNDS + LAID) // 2
        back = []
        round_across(0, 0, slice(0, 1))
        round_last(VECTOR_ROUNDS, middle)
        round_across(0, 0, slice(1, 2))
        round_last(middle, LAID)
        for k in groups:
            if k > 0:
                round_across(0, k, slice(0, 2))
            back.append(psum.tile([P, 2, 2, P], F32, name="back%d" % k, tag=free_banks[0][k]))
            turn_back(0, k)
        for k in groups:
            round_across(1, k, slice(0, 2))
            turn_back(1, k)
        for k in groups[:-1]:
            weave_back(k, slice(0, 2))
        for b in range(2):
            weave_back(groups[-1], slice(b, b + 1))

        def lay(copy, first, stop):
            copy(
                out=o_bf[:, first:stop, :].rearrange("p (c i) j -> p c j i", i=4),
                in_=rounded[:, :, first:stop].rearrange("p j (c i) -> p c j i", i=4),
            )

        lay(nc.vector.tensor_copy, *pieces[0])
        stored = 0
        for k, (first, stop) in enumerate(pieces):
            if stop < LAID:
                lay(nc.vector.tensor_copy, stop, min(stop + PIECE, LAID))
            group, column = divmod(first, SCALE_GROUP)
            nc.vector.quantize_mx(
                out=o_codes[:, first:stop].bitcast(E4M3),
                scales=o_scales[4 * group :, column : column + stop - first],
                in_=o_bf[:, first:stop, :].rearrange("p c j -> p (c j)"),
            )
            if stop in WORD_STORE_ENDS:
                nc.sync.dma_start(out=out_words[:, stored:stop], in_=o_codes[:, stored:stop].bitcast(I32))
                stored = stop
        for quadrant in range(4):
            queue = nc.sync if quadrant % 2 else nc.scalar
            rows = out_2[0, 4 * quadrant : 4 * quadrant + 4, :].bitcast(I32).rearrange("r (k c) -> k r c", k=4)
            queue.dma_start(out=rows, in_=o_scales[32 * quadrant : 32 * quadrant + 16, :].bitcast(I32))
